import numpy as np
import ml_dtypes


def mxq(x, axis, fmt="e4m3"):
    dtype, down = {"e4m3": (ml_dtypes.float8_e4m3fn, 7), "e5m2": (ml_dtypes.float8_e5m2, 14)}[fmt]
    v = np.moveaxis(np.asarray(x, np.float32).astype(ml_dtypes.bfloat16).astype(np.float64), axis, -1)
    blocks = v.reshape(v.shape[:-1] + (-1, 32))
    amax = np.abs(blocks).max(-1, keepdims=True)
    byte = np.maximum(np.where(amax > 0, np.frexp(amax)[1] - 1 + 127, 0) - down, 1)
    scale = np.exp2(byte - 127.0)
    codes = (blocks / scale).astype(np.float32).astype(dtype).astype(np.float64)
    return np.moveaxis((codes * scale).reshape(v.shape), -1, axis)


WIDE = False


def mx_kscale(k):
    if not WIDE:
        return np.ones(k)
    levels = np.array([10, -10, 5, -5, 0])
    if k % 512:
        return np.exp2(np.random.permutation(np.resize(levels, k // 32))).repeat(32)
    a = np.empty((k // 512, 16))
    for p in range(k // 512):
        a[p, :8] = np.random.permutation(np.resize(levels, 8))
        for g in range(8):
            far = levels[np.abs(levels - a[p, g]) >= 10]
            a[p, g + 8] = far[np.random.randint(len(far))]
    return np.exp2(a.ravel()).repeat(32)


def f64(x):
    return np.asarray(x).astype(np.float64)


def striped(idx):
    return np.tile(idx.reshape(-1, 16).T, (8, 1)).astype(np.uint16)


def unstriped(offs):
    return offs[:16].T.reshape(-1).astype(np.int64)


def pack_weight(w):
    k, n = w.shape
    w = f64(np.asarray(w, np.float32).astype(ml_dtypes.bfloat16)).reshape(k // 32, 32, n)
    amax = np.abs(w).max(1)
    byte = np.clip(np.where(amax > 0, np.frexp(amax)[1] - 1 + 127 - 7, 1), 1, 254)
    scaled = (w * np.exp2(127.0 - byte)[:, None, :]).reshape(k, n).astype(np.float32)
    words = np.ascontiguousarray(scaled.reshape(k // 512, 128, 4, n).transpose(0, 1, 3, 2)).astype(ml_dtypes.float8_e4m3fn).view(np.uint8)
    return words, np.ascontiguousarray(byte.astype(np.uint8).reshape(k // 512, 16, n))


def unpack_weight(words, scales):
    g, p, n, _ = words.shape
    vals = np.ascontiguousarray(words).view(ml_dtypes.float8_e4m3fn).astype(np.float64) * np.repeat(np.exp2(scales.astype(np.float64) - 127.0), 8, axis=1)[..., None]
    return vals.transpose(0, 1, 3, 2).reshape(g * 512, n)


K, T, S, H, N, U = 1024, 2048, 512, 512, 128, 1024


def setup_inputs():
    n = np.random.standard_normal
    s = mx_kscale(K)[:, None]
    u = mx_kscale(H)
    packed_xT = pack_weight(n((K, T)) * s)
    packed_w2 = pack_weight(n((H, N)) / np.sqrt(H) / u[:, None])
    return {
        "x_words": packed_xT[0],
        "x_scales": packed_xT[1],
        "w1": (n((K, H)) / np.sqrt(K) / s * u).astype(np.float32),
        "w2_words": packed_w2[0],
        "w2_scales": packed_w2[1],
        "skip": (n((H, U)) * u[:, None]).astype(np.float32),
        "offs": striped(np.random.permutation(T)[:S]),
        "cell": striped(np.random.permutation(U)[:S]),
    }


def reference(x_words, x_scales, w1, w2_words, w2_scales, skip, offs, cell):
    xq = unpack_weight(x_words, x_scales)[:, unstriped(offs)]
    up = np.zeros((H, U))
    up[:, unstriped(cell)] = mxq(f64(w1), 0, "e4m3").T @ xq
    z = up + f64(skip)
    return unpack_weight(w2_words, w2_scales).T @ mxq(z, 0, "e4m3")

@@ -1,0 +1,243 @@
+from contextlib import ExitStack
+
+import concourse.mybir as mybir
+from concourse.masks import make_identity
+
+K, T, S, H, N, U = 1024, 2048, 512, 512, 128, 1024
+FLOPS = 2 * K * H * S + 2 * H * N * U
+
+F32 = mybir.dt.float32
+BF16 = mybir.dt.bfloat16
+I32 = mybir.dt.int32
+U32 = mybir.dt.uint32
+U16 = mybir.dt.uint16
+U8 = mybir.dt.uint8
+FP8X4 = mybir.dt.float8_e4m3fn_x4
+
+P = 128
+PACK = 4
+K_PASSES = K // (P * PACK)
+ROW_TILES = H // P
+HALF = S // 2
+LIST_COLS = S // 16
+HALF_COLS = LIST_COLS // 2
+SIDE = U // 2
+PAIR = 2 * P
+
+
+def tile_picked_unet_none_p_kernel(
+    tc, x_words, x_scales, w1, w2_words, w2_scales, skip, offs, cell, out
+):
+    nc = tc.nc
+    with ExitStack() as ctx:
+        lists = ctx.enter_context(tc.tile_pool(name="lists", bufs=1))
+        keep = ctx.enter_context(tc.tile_pool(name="keep", bufs=1))
+        psum = ctx.enter_context(tc.psum_pool(name="psum", bufs=2))
+
+        offs_sb = lists.tile([P, LIST_COLS], U16, name="offs_sb")
+        cell_sb = lists.tile([P, LIST_COLS], U16, name="cell_sb")
+
+        x_table = [keep.tile([P, T], U32, name=f"x_table{g}", align_bytes=64) for g in range(K_PASSES)]
+        xs_table = keep.tile([P, T], U8, align_bytes=64)
+        x_picked = [keep.tile([P, S], U32, name=f"x_picked{g}", align_bytes=64) for g in range(K_PASSES)]
+        xs_picked = keep.tile([P, S], U8, align_bytes=64)
+        w1_raw = [
+            [keep.tile([P, PACK, P], F32, name=f"w1_raw{b}_{g}", tag=f"w1_raw{b}_{g}", align_bytes=64) for g in range(K_PASSES)]
+            for b in range(ROW_TILES)
+        ]
+        skip_sb = [keep.tile([P, U], F32, name=f"skip{b}", align_bytes=64) for b in range(ROW_TILES)]
+        up = [keep.tile([P, U], F32, name=f"up{b}", align_bytes=64) for b in range(ROW_TILES)]
+        w2_codes = keep.tile([P, 2, 2, N], U32, align_bytes=64)
+        w2_plane = keep.tile([P, 2, N], U8, align_bytes=64)
+        ident = keep.tile([P, P], F32, align_bytes=64)
+
+        nc.vector.memset(xs_table[:].bitcast(I32), 0)
+        for b in range(2):
+            nc.vector.memset(up[b][:], 0.0)
+            nc.scalar.copy(out=up[b + 2][:], in_=up[b][:])
+        nc.vector.memset(w2_codes[:].bitcast(I32), 0)
+        nc.vector.memset(w2_plane[:].bitcast(I32), 0)
+        make_identity(nc, ident[:])
+
+        w1_rows = w1.rearrange("(g p j) c -> g p j c", g=K_PASSES, j=PACK)
+        x_rows = x_words.rearrange("g p n t -> g p (n t)").bitcast(I32)
+        xs_rows = x_scales.bitcast(I32)
+
+        def load_w1(b):
+            for g in range(K_PASSES):
+                nc.sync.dma_start(out=w1_raw[b][g][:], in_=w1_rows[g, :, :, b * P : (b + 1) * P])
+
+        nc.sync.dma_start(offs_sb[:], offs)
+        nc.sync.dma_start(out=x_table[0][:].bitcast(I32), in_=x_rows[0])
+        for q in range(4):
+            nc.sync.dma_start(
+                out=xs_table[32 * q : 32 * q + 4 * K_PASSES, :].bitcast(I32), in_=xs_rows[:, 4 * q : 4 * q + 4, :]
+            )
+        load_w1(0)
+        nc.sync.dma_start(out=x_table[1][:].bitcast(I32), in_=x_rows[1])
+        nc.sync.dma_start(cell_sb[:], cell)
+        for b in range(ROW_TILES):
+            if b + 1 < ROW_TILES:
+                load_w1(b + 1)
+            nc.sync.dma_start(out=skip_sb[b][:], in_=skip[b * P : (b + 1) * P, :])
+        w2_rows = w2_words[0].rearrange("(s p) n t -> p s (n t)", s=2).bitcast(I32)
+        for side in range(2):
+            nc.sync.dma_start(out=w2_codes[64 * side : 64 * side + 64, side, :, :].bitcast(I32), in_=w2_rows)
+        w2s_rows = w2_scales[0].rearrange("(s a r) n -> a r s n", s=2, a=2).bitcast(I32)
+        for q in range(4):
+            nc.sync.dma_start(out=w2_plane[32 * q : 32 * q + 4, :, :].bitcast(I32), in_=w2s_rows[q % 2])
+
+        def list_part(tile, part):
+            return tile[:, part.start // 16 : part.stop // 16]
+
+        def quantise_w1(b):
+            grouped = keep.tile([P, K_PASSES * P * PACK], BF16, name=f"w1_bf{b}", align_bytes=64)
+            for g in range(K_PASSES):
+                nc.scalar.copy(
+                    out=grouped[:, g * P * PACK : (g + 1) * P * PACK].rearrange("p (c i j) -> p c j i", i=4, j=PACK),
+                    in_=w1_raw[b][g][:].rearrange("p j (c i) -> p c j i", i=4),
+                )
+            codes = keep.tile([P, K_PASSES * P], U32, name=f"w1_codes{b}", align_bytes=64)
+            plane = keep.tile([P, K_PASSES * P], U8, name=f"w1_plane{b}", align_bytes=64)
+            nc.vector.quantize_mx(out=codes[:].bitcast(FP8X4), scales=plane[:], in_=grouped[:])
+            return codes, plane
+
+        def first_product(w1_q, part):
+            codes, plane = w1_q
+            acc = psum.tile([P, part.stop - part.start], F32, name="h_acc", tag="mm")
+            edges = [part.start] + [e for e in (HALF,) if part.start < e < part.stop] + [part.stop]
+            for lo, hi in zip(edges, edges[1:]):
+                for g in range(K_PASSES):
+                    nc.tensor.matmul_mx(
+                        out=acc[:, lo - part.start : hi - part.start],
+                        lhsT=codes[:, g * P : (g + 1) * P].bitcast(FP8X4),
+                        lhsT_scale=plane[:, g * P : (g + 1) * P],
+                        rhs=x_picked[g][:, lo:hi].bitcast(FP8X4),
+                        rhs_scale=xs_picked[4 * g : P, lo:hi],
+                        start=(g == 0),
+                        stop=(g == K_PASSES - 1),
+                    )
+            return acc
+
+        def leave_psum(acc, part, tag):
+            h = keep.tile([P, part.stop - part.start], F32, name="h", tag=tag, align_bytes=64)
+            nc.scalar.copy(out=h[:], in_=acc[:])
+            return h
+
+        def scatter(b, part, h):
+            nc.vector.tensor_copy(up[b][:].indirect(list_part(cell_sb, part)), h[:])
+
+        z_turned = [
+            [keep.tile([P, PACK * P], BF16, name=f"z_turned{s}_{j}", tag=f"z_turned{s}_{j}", align_bytes=64) for j in range(4)]
+            for s in range(2)
+        ]
+
+        def turn(banks, source, first):
+            for bank, blocks in banks:
+                for n, j in enumerate(blocks):
+                    for side in range(2):
+                        col = side * SIDE + j * P
+                        nc.tensor.matmul(
+                            out=bank[:, n, side, :],
+                            lhsT=source[:, col : col + P],
+                            rhs=ident[:],
+                            is_transpose=True,
+                            start=(first and n == 0 and side == 0),
+                            stop=(not first and n == len(blocks) - 1 and side == 1),
+                        )
+
+        def turn_skip(b, per_bank):
+            banks = [
+                (psum.tile([P, per_bank, 2, P], F32, name="z_bank", tag="turn", bufs=4), range(j, j + per_bank))
+                for j in range(0, 4, per_bank)
+            ]
+            turn(banks, skip_sb[b], True)
+            return banks
+
+        def add_up(b, banks, movers):
+            turn(banks, up[b], False)
+            for bank, blocks in banks:
+                for n, j in enumerate(blocks):
+                    movers[j % 2](
+                        out=z_turned[b // 2][j][:].rearrange("q (u s f a e) -> q f s u a e", u=2, s=2, f=2, e=2)[:, b % 2],
+                        in_=bank[:, n].rearrange("q s (a u e) -> q s u a e", u=2, e=2),
+                    )
+
+        def turn_back(s, per_tile):
+            grouped = [
+                keep.tile([P, per_tile * P * PACK], BF16, name=f"z_bf{s}_{j}", align_bytes=64) for j in range(0, 4, per_tile)
+            ]
+            for j in range(4):
+                bank = psum.tile([P, 2, P], F32, name="back_bank", tag="back")
+                words = z_turned[s][j][:].bitcast(F32)
+                for u in range(2):
+                    nc.tensor.transpose(bank[:, u, :], words[:, u * P : (u + 1) * P], ident[:])
+                at = (j % per_tile) * 2 * P
+                nc.scalar.copy(
+                    out=grouped[j // per_tile][:].bitcast(F32)[:, at : at + 2 * P].rearrange("p (q u) -> p q u", u=2),
+                    in_=bank[:].rearrange("p u q -> p q u"),
+                )
+            return grouped
+
+        def quantise_z(s, grouped):
+            codes = keep.tile([P, SIDE], U32, name=f"z_codes{s}", align_bytes=64)
+            plane = keep.tile([P, SIDE], U8, name=f"z_plane{s}", align_bytes=64)
+            width = SIDE // len(grouped)
+            parts = [slice(lo, lo + width) for lo in range(0, SIDE, width)]
+            for cols, z_bf in zip(parts, grouped):
+                nc.vector.quantize_mx(out=codes[:, cols].bitcast(FP8X4), scales=plane[:, cols], in_=z_bf[:])
+            return codes, plane, parts
+
+        def second_product(s, z_q, accs):
+            codes, plane, parts = z_q
+            for cols in parts:
+                for side in range(2):
+                    nc.tensor.matmul_mx(
+                        out=accs[side][:, cols],
+                        lhsT=w2_codes[:, side, s, :].bitcast(FP8X4),
+                        lhsT_scale=w2_plane[:, s, :],
+                        rhs=codes[:, cols].bitcast(FP8X4),
+                        rhs_scale=plane[:, cols],
+                        start=(s == 0),
+                        stop=(s == 1 and cols.stop == SIDE),
+                    )
+
+        nc.vector.tensor_copy(x_picked[0][:], x_table[0][:].indirect(offs_sb[:]))
+        nc.vector.tensor_copy(xs_picked[:], xs_table[:].indirect(offs_sb[:]))
+        w1_q = quantise_w1(0)
+        for part in (slice(0, HALF), slice(HALF, S)):
+            nc.vector.tensor_copy(x_picked[1][:, part], x_table[1][:].indirect(list_part(offs_sb, part)))
+
+        on_scalar = (nc.scalar.copy, nc.scalar.copy)
+        last = ROW_TILES - 1
+
+        def parts_of(b):
+            edge = HALF if b == last else P
+            return slice(0, edge), slice(edge, S)
+
+        accs = [first_product(w1_q, part) for part in parts_of(0)]
+        for b in range(ROW_TILES):
+            head, rest = parts_of(b)
+            scatter(b, head, leave_psum(accs[0], head, f"h{b}"))
+            if b < last:
+                w1_q = quantise_w1(b + 1)
+                spent = f"w1_raw{b + 1}_{K_PASSES - 1}"
+            else:
+                z_q = quantise_z(0, low_rows)
+                spent = "z_turned0_3"
+            scatter(b, rest, leave_psum(accs[1], rest, spent))
+            if b < last:
+                accs = [first_product(w1_q, part) for part in parts_of(b + 1)]
+                add_up(b, turn_skip(b, 2), on_scalar)
+            if b == 1:
+                low_rows = turn_back(0, 4)
+
+        banks = turn_skip(last, 1)
+        accs = [psum.tile([P, SIDE], F32, name="out_acc", tag="mm") for side in range(2)]
+        second_product(0, z_q, accs)
+        add_up(last, banks, (nc.scalar.copy, nc.vector.tensor_copy))
+        second_product(1, quantise_z(1, turn_back(1, 1)), accs)
+        for side, mover in enumerate((nc.scalar.copy, nc.vector.tensor_copy)):
+            result = keep.tile([P, SIDE], F32, name=f"result{side}")
+            mover(out=result[:], in_=accs[side][:])
+            nc.sync.dma_start(out=out[:, side * SIDE : (side + 1) * SIDE], in_=result[:])

@@ -52,9 +52,9 @@ def tile_picked_unet_none_p_kernel(
         ident = keep.tile([P, P], F32, align_bytes=64)
 
         nc.vector.memset(xs_table[:].bitcast(I32), 0)
-        for b in range(2):
-            nc.vector.memset(up[b][:], 0.0)
-            nc.scalar.copy(out=up[b + 2][:], in_=up[b][:])
+        nc.vector.memset(up[0][:], 0.0)
+        for b in range(1, ROW_TILES):
+            nc.scalar.copy(out=up[b][:], in_=up[0][:])
         nc.vector.memset(w2_codes[:].bitcast(I32), 0)
         nc.vector.memset(w2_plane[:].bitcast(I32), 0)
         make_identity(nc, ident[:])
@@ -67,8 +67,8 @@ def tile_picked_unet_none_p_kernel(
             for g in range(K_PASSES):
                 nc.sync.dma_start(out=w1_raw[b][g][:], in_=w1_rows[g, :, :, b * P : (b + 1) * P])
 
-        nc.sync.dma_start(offs_sb[:], offs)
         nc.sync.dma_start(out=x_table[0][:].bitcast(I32), in_=x_rows[0])
+        nc.sync.dma_start(offs_sb[:], offs)
         for q in range(4):
             nc.sync.dma_start(
                 out=xs_table[32 * q : 32 * q + 4 * K_PASSES, :].bitcast(I32), in_=xs_rows[:, 4 * q : 4 * q + 4, :]
@@ -119,9 +119,9 @@ def tile_picked_unet_none_p_kernel(
                     )
             return acc
 
-        def leave_psum(acc, part, tag):
+        def leave_psum(acc, part, tag, mover=nc.scalar.copy):
             h = keep.tile([P, part.stop - part.start], F32, name="h", tag=tag, align_bytes=64)
-            nc.scalar.copy(out=h[:], in_=acc[:])
+            mover(out=h[:], in_=acc[:])
             return h
 
         def scatter(b, part, h):
@@ -163,12 +163,12 @@ def tile_picked_unet_none_p_kernel(
                         in_=bank[:, n].rearrange("q s (a u e) -> q s u a e", u=2, e=2),
                     )
 
-        def turn_back(s, per_tile):
+        def turn_back(s, per_tile, tags):
             grouped = [
                 keep.tile([P, per_tile * P * PACK], BF16, name=f"z_bf{s}_{j}", align_bytes=64) for j in range(0, 4, per_tile)
             ]
             for j in range(4):
-                bank = psum.tile([P, 2, P], F32, name="back_bank", tag="back")
+                bank = psum.tile([P, 2, P], F32, name="back_bank", tag=tags[j // 2])
                 words = z_turned[s][j][:].bitcast(F32)
                 for u in range(2):
                     nc.tensor.transpose(bank[:, u, :], words[:, u * P : (u + 1) * P], ident[:])
@@ -186,21 +186,19 @@ def tile_picked_unet_none_p_kernel(
             parts = [slice(lo, lo + width) for lo in range(0, SIDE, width)]
             for cols, z_bf in zip(parts, grouped):
                 nc.vector.quantize_mx(out=codes[:, cols].bitcast(FP8X4), scales=plane[:, cols], in_=z_bf[:])
-            return codes, plane, parts
+            return codes, plane
 
-        def second_product(s, z_q, accs):
-            codes, plane, parts = z_q
-            for cols in parts:
-                for side in range(2):
-                    nc.tensor.matmul_mx(
-                        out=accs[side][:, cols],
-                        lhsT=w2_codes[:, side, s, :].bitcast(FP8X4),
-                        lhsT_scale=w2_plane[:, s, :],
-                        rhs=codes[:, cols].bitcast(FP8X4),
-                        rhs_scale=plane[:, cols],
-                        start=(s == 0),
-                        stop=(s == 1 and cols.stop == SIDE),
-                    )
+        def second_product(s, z_q, cols, side, acc, start, stop):
+            codes, plane = z_q
+            nc.tensor.matmul_mx(
+                out=acc,
+                lhsT=w2_codes[:, side, s, :].bitcast(FP8X4),
+                lhsT_scale=w2_plane[:, s, :],
+                rhs=codes[:, cols].bitcast(FP8X4),
+                rhs_scale=plane[:, cols],
+                start=start,
+                stop=stop,
+            )
 
         nc.vector.tensor_copy(x_picked[0][:], x_table[0][:].indirect(offs_sb[:]))
         nc.vector.tensor_copy(xs_picked[:], xs_table[:].indirect(offs_sb[:]))
@@ -211,33 +209,34 @@ def tile_picked_unet_none_p_kernel(
         on_scalar = (nc.scalar.copy, nc.scalar.copy)
         last = ROW_TILES - 1
 
-        def parts_of(b):
-            edge = HALF if b == last else P
-            return slice(0, edge), slice(edge, S)
+        parts = slice(0, P), slice(P, S)
 
-        accs = [first_product(w1_q, part) for part in parts_of(0)]
-        for b in range(ROW_TILES):
-            head, rest = parts_of(b)
-            scatter(b, head, leave_psum(accs[0], head, f"h{b}"))
-            if b < last:
-                w1_q = quantise_w1(b + 1)
-                spent = f"w1_raw{b + 1}_{K_PASSES - 1}"
-            else:
-                z_q = quantise_z(0, low_rows)
-                spent = "z_turned0_3"
-            scatter(b, rest, leave_psum(accs[1], rest, spent))
-            if b < last:
-                accs = [first_product(w1_q, part) for part in parts_of(b + 1)]
-                add_up(b, turn_skip(b, 2), on_scalar)
+        accs = [first_product(w1_q, part) for part in parts]
+        for b in range(last):
+            scatter(b, parts[0], leave_psum(accs[0], parts[0], f"h{b}", nc.scalar.copy if b else nc.vector.tensor_copy))
+            w1_q = quantise_w1(b + 1)
+            scatter(b, parts[1], leave_psum(accs[1], parts[1], f"w1_raw{b + 1}_{K_PASSES - 1}"))
+            accs = [first_product(w1_q, part) for part in parts]
+            add_up(b, turn_skip(b, 2), on_scalar)
             if b == 1:
-                low_rows = turn_back(0, 4)
+                low_rows = turn_back(0, 4, ("back", "back"))
+        for n, part in enumerate(parts):
+            scatter(last, part, leave_psum(accs[n], part, f"h{last}_{n}"))
 
         banks = turn_skip(last, 1)
-        accs = [psum.tile([P, SIDE], F32, name="out_acc", tag="mm") for side in range(2)]
-        second_product(0, z_q, accs)
+        low_q = quantise_z(0, low_rows)
         add_up(last, banks, (nc.scalar.copy, nc.vector.tensor_copy))
-        second_product(1, quantise_z(1, turn_back(1, 1)), accs)
-        for side, mover in enumerate((nc.scalar.copy, nc.vector.tensor_copy)):
-            result = keep.tile([P, SIDE], F32, name=f"result{side}")
-            mover(out=result[:], in_=accs[side][:])
-            nc.sync.dma_start(out=out[:, side * SIDE : (side + 1) * SIDE], in_=result[:])
+        high_q = quantise_z(1, turn_back(1, 1, ("back", "mm")))
+        for jp in range(2):
+            accs = [psum.tile([P, PAIR], F32, name="out_acc", tag=("back", "mm")[jp]) for side in range(2)]
+            for side in range(2):
+                second_product(0, low_q, slice(jp * PAIR, (jp + 1) * PAIR), side, accs[side][:], True, False)
+            for n in range(2):
+                for side in range(2):
+                    lo = jp * PAIR + n * P
+                    second_product(1, high_q, slice(lo, lo + P), side, accs[side][:, n * P : (n + 1) * P], False, n == 1)
+            for side, mover in enumerate((nc.scalar.copy, nc.vector.tensor_copy)):
+                result = keep.tile([P, PAIR], F32, name=f"result{side}_{jp}")
+                mover(out=result[:], in_=accs[side][:])
+                lo = side * SIDE + jp * PAIR
+                nc.sync.dma_start(out=out[:, lo : lo + PAIR], in_=result[:])

@@ -32,6 +32,7 @@ def tile_picked_unet_none_p_kernel(
     with ExitStack() as ctx:
         lists = ctx.enter_context(tc.tile_pool(name="lists", bufs=1))
         keep = ctx.enter_context(tc.tile_pool(name="keep", bufs=1))
+        shared = ctx.enter_context(tc.tile_pool(name="shared", bufs=1))
         psum = ctx.enter_context(tc.psum_pool(name="psum", bufs=2))
 
         offs_sb = lists.tile([P, LIST_COLS], U16, name="offs_sb")
@@ -43,8 +44,14 @@ def tile_picked_unet_none_p_kernel(
         xs_picked = keep.tile([P, S], U8, align_bytes=64)
         w1_raw = [
             [keep.tile([P, PACK, P], F32, name=f"w1_raw{b}_{g}", tag=f"w1_raw{b}_{g}", align_bytes=64) for g in range(K_PASSES)]
-            for b in range(ROW_TILES)
+            for b in range(ROW_TILES - 1)
         ]
+        w1_raw.append(
+            [
+                keep.tile([P, PACK, P], F32, name="w1_raw3_0", align_bytes=64),
+                shared.tile([P, PACK, P], F32, name="w1_raw3_1", offset=0, align_bytes=64),
+            ]
+        )
         skip_sb = [keep.tile([P, U], F32, name=f"skip{b}", align_bytes=64) for b in range(ROW_TILES)]
         up = [keep.tile([P, U], F32, name=f"up{b}", align_bytes=64) for b in range(ROW_TILES)]
         w2_codes = keep.tile([P, 2, 2, N], U32, align_bytes=64)
@@ -76,10 +83,12 @@ def tile_picked_unet_none_p_kernel(
         load_w1(0)
         nc.sync.dma_start(out=x_table[1][:].bitcast(I32), in_=x_rows[1])
         nc.sync.dma_start(cell_sb[:], cell)
+        load_w1(1)
         for b in range(ROW_TILES):
-            if b + 1 < ROW_TILES:
-                load_w1(b + 1)
             nc.sync.dma_start(out=skip_sb[b][:], in_=skip[b * P : (b + 1) * P, :])
+            if b == 0:
+                load_w1(2)
+                load_w1(3)
         w2_rows = w2_words[0].rearrange("(s p) n t -> p s (n t)", s=2).bitcast(I32)
         for side in range(2):
             nc.sync.dma_start(out=w2_codes[64 * side : 64 * side + 64, side, :, :].bitcast(I32), in_=w2_rows)
@@ -102,10 +111,10 @@ def tile_picked_unet_none_p_kernel(
             nc.vector.quantize_mx(out=codes[:].bitcast(FP8X4), scales=plane[:], in_=grouped[:])
             return codes, plane
 
-        def first_product(w1_q, part):
+        def first_product(w1_q, part, tag):
             codes, plane = w1_q
-            acc = psum.tile([P, part.stop - part.start], F32, name="h_acc", tag="mm")
-            edges = [part.start] + [e for e in (HALF,) if part.start < e < part.stop] + [part.stop]
+            acc = psum.tile([P, part.stop - part.start], F32, name="h_acc", tag=tag)
+            edges = [part.start] + ([HALF] if part.start == P else []) + [part.stop]
             for lo, hi in zip(edges, edges[1:]):
                 for g in range(K_PASSES):
                     nc.tensor.matmul_mx(
@@ -119,18 +128,17 @@ def tile_picked_unet_none_p_kernel(
                     )
             return acc
 
-        def leave_psum(acc, part, tag, mover=nc.scalar.copy):
-            h = keep.tile([P, part.stop - part.start], F32, name="h", tag=tag, align_bytes=64)
+        def leave_psum(acc, h, mover=nc.scalar.copy):
             mover(out=h[:], in_=acc[:])
             return h
+
+        def h_tile(part, tag):
+            return keep.tile([P, part.stop - part.start], F32, name="h", tag=tag, align_bytes=64)
 
         def scatter(b, part, h):
             nc.vector.tensor_copy(up[b][:].indirect(list_part(cell_sb, part)), h[:])
 
-        z_turned = [
-            [keep.tile([P, PACK * P], BF16, name=f"z_turned{s}_{j}", tag=f"z_turned{s}_{j}", align_bytes=64) for j in range(4)]
-            for s in range(2)
-        ]
+        z_turned = []
 
         def turn(banks, source, first):
             for bank, blocks in banks:
@@ -146,10 +154,11 @@ def tile_picked_unet_none_p_kernel(
                             stop=(not first and n == len(blocks) - 1 and side == 1),
                         )
 
-        def turn_skip(b, per_bank):
+        def turn_skip(b, tags):
+            per_bank = 4 // len(tags)
             banks = [
-                (psum.tile([P, per_bank, 2, P], F32, name="z_bank", tag="turn", bufs=4), range(j, j + per_bank))
-                for j in range(0, 4, per_bank)
+                (psum.tile([P, per_bank, 2, P], F32, name="z_bank", tag=tag), range(n * per_bank, (n + 1) * per_bank))
+                for n, tag in enumerate(tags)
             ]
             turn(banks, skip_sb[b], True)
             return banks
@@ -159,7 +168,7 @@ def tile_picked_unet_none_p_kernel(
             for bank, blocks in banks:
                 for n, j in enumerate(blocks):
                     movers[j % 2](
-                        out=z_turned[b // 2][j][:].rearrange("q (u s f a e) -> q f s u a e", u=2, s=2, f=2, e=2)[:, b % 2],
+                        out=z_turned[b // 2][j].rearrange("q (u s f a e) -> q f s u a e", u=2, s=2, f=2, e=2)[:, b % 2],
                         in_=bank[:, n].rearrange("q s (a u e) -> q s u a e", u=2, e=2),
                     )
 
@@ -169,7 +178,7 @@ def tile_picked_unet_none_p_kernel(
             ]
             for j in range(4):
                 bank = psum.tile([P, 2, P], F32, name="back_bank", tag=tags[j // 2])
-                words = z_turned[s][j][:].bitcast(F32)
+                words = z_turned[s][j].bitcast(F32)
                 for u in range(2):
                     nc.tensor.transpose(bank[:, u, :], words[:, u * P : (u + 1) * P], ident[:])
                 at = (j % per_tile) * 2 * P
@@ -209,26 +218,40 @@ def tile_picked_unet_none_p_kernel(
         on_scalar = (nc.scalar.copy, nc.scalar.copy)
         last = ROW_TILES - 1
 
-        parts = slice(0, P), slice(P, S)
+        short, rest = slice(0, P), slice(P, S)
+        halves = slice(0, HALF), slice(HALF, S)
+        whole = slice(0, S)
 
-        accs = [first_product(w1_q, part) for part in parts]
-        for b in range(last):
-            scatter(b, parts[0], leave_psum(accs[0], parts[0], f"h{b}", nc.scalar.copy if b else nc.vector.tensor_copy))
-            w1_q = quantise_w1(b + 1)
-            scatter(b, parts[1], leave_psum(accs[1], parts[1], f"w1_raw{b + 1}_{K_PASSES - 1}"))
-            accs = [first_product(w1_q, part) for part in parts]
-            add_up(b, turn_skip(b, 2), on_scalar)
-            if b == 1:
-                low_rows = turn_back(0, 4, ("back", "back"))
-        for n, part in enumerate(parts):
-            scatter(last, part, leave_psum(accs[n], part, f"h{last}_{n}"))
+        accs = [first_product(w1_q, part, "a") for part in (short, rest)]
+        scatter(0, short, leave_psum(accs[0], h_tile(short, "h0"), nc.vector.tensor_copy))
+        w1_q = quantise_w1(1)
+        scatter(0, rest, leave_psum(accs[1], h_tile(rest, "w1_raw1_1")))
 
-        banks = turn_skip(last, 1)
+        accs = [first_product(w1_q, part, "a") for part in halves]
+        scatter(1, halves[0], leave_psum(accs[0], h_tile(halves[0], "h1")))
+        late_q = [quantise_w1(b) for b in (2, 3)]
+        h_held = shared.tile([P, HALF], F32, name="h_held", offset=0, align_bytes=64)
+        scatter(1, halves[1], leave_psum(accs[1], h_held))
+
+        accs = [first_product(late_q[0], part, "a") for part in (short, rest)]
+        acc_last = first_product(late_q[1], whole, "d")
+        for n, part in enumerate((short, rest)):
+            scatter(2, part, leave_psum(accs[n], h_tile(part, f"h2_{n}")))
+        scatter(last, whole, leave_psum(acc_last, h_tile(whole, "h3")))
+
+        z_low = shared.tile([P, 4 * PACK * P], BF16, name="z_low", offset=HALF * 4, align_bytes=64)
+        z_turned.append([z_low[:, j * PACK * P : (j + 1) * PACK * P] for j in range(4)])
+        z_turned.append([keep.tile([P, PACK * P], BF16, name=f"z_high{j}", align_bytes=64)[:] for j in range(4)])
+        add_up(0, turn_skip(0, "bb"), on_scalar)
+        add_up(1, turn_skip(1, "cc"), on_scalar)
+        low_rows = turn_back(0, 4, "dd")
+        banks = [turn_skip(2, "bb"), turn_skip(last, "aacc")]
+        add_up(2, banks[0], on_scalar)
         low_q = quantise_z(0, low_rows)
-        add_up(last, banks, (nc.scalar.copy, nc.vector.tensor_copy))
-        high_q = quantise_z(1, turn_back(1, 1, ("back", "mm")))
+        add_up(last, banks[1], (nc.scalar.copy, nc.vector.tensor_copy))
+        high_q = quantise_z(1, turn_back(1, 1, "db"))
         for jp in range(2):
-            accs = [psum.tile([P, PAIR], F32, name="out_acc", tag=("back", "mm")[jp]) for side in range(2)]
+            accs = [psum.tile([P, PAIR], F32, name="out_acc", tag="db"[jp]) for side in range(2)]
             for side in range(2):
                 second_product(0, low_q, slice(jp * PAIR, (jp + 1) * PAIR), side, accs[side][:], True, False)
             for n in range(2):

@@ -13,6 +13,7 @@ U32 = mybir.dt.uint32
 U16 = mybir.dt.uint16
 U8 = mybir.dt.uint8
 FP8X4 = mybir.dt.float8_e4m3fn_x4
+COPY = mybir.ActivationFunctionType.Copy
 
 P = 128
 PACK = 4
@@ -20,9 +21,9 @@ K_PASSES = K // (P * PACK)
 ROW_TILES = H // P
 HALF = S // 2
 LIST_COLS = S // 16
-HALF_COLS = LIST_COLS // 2
 SIDE = U // 2
 PAIR = 2 * P
+SHARE = 128
 
 
 def tile_picked_unet_none_p_kernel(
@@ -32,8 +33,7 @@ def tile_picked_unet_none_p_kernel(
     with ExitStack() as ctx:
         lists = ctx.enter_context(tc.tile_pool(name="lists", bufs=1))
         keep = ctx.enter_context(tc.tile_pool(name="keep", bufs=1))
-        shared = ctx.enter_context(tc.tile_pool(name="shared", bufs=1))
-        psum = ctx.enter_context(tc.psum_pool(name="psum", bufs=2))
+        psum = ctx.enter_context(tc.psum_pool(name="psum", bufs=1))
 
         offs_sb = lists.tile([P, LIST_COLS], U16, name="offs_sb")
         cell_sb = lists.tile([P, LIST_COLS], U16, name="cell_sb")
@@ -42,17 +42,14 @@ def tile_picked_unet_none_p_kernel(
         xs_table = keep.tile([P, T], U8, align_bytes=64)
         x_picked = [keep.tile([P, S], U32, name=f"x_picked{g}", align_bytes=64) for g in range(K_PASSES)]
         xs_picked = keep.tile([P, S], U8, align_bytes=64)
+        widths = (P, P, PAIR)
         w1_raw = [
-            [keep.tile([P, PACK, P], F32, name=f"w1_raw{b}_{g}", tag=f"w1_raw{b}_{g}", align_bytes=64) for g in range(K_PASSES)]
-            for b in range(ROW_TILES - 1)
+            [keep.tile([P, PACK, w], F32, name=f"w1_raw{n}_{g}", tag=f"w1_raw{n}_{g}", align_bytes=64) for g in range(K_PASSES)]
+            for n, w in enumerate(widths)
         ]
-        w1_raw.append(
-            [
-                keep.tile([P, PACK, P], F32, name="w1_raw3_0", align_bytes=64),
-                shared.tile([P, PACK, P], F32, name="w1_raw3_1", offset=0, align_bytes=64),
-            ]
-        )
-        skip_sb = [keep.tile([P, U], F32, name=f"skip{b}", align_bytes=64) for b in range(ROW_TILES)]
+        skip_first = keep.tile([P, U], F32, align_bytes=64)
+        skip_rest = keep.tile([P, ROW_TILES - 1, U], F32, align_bytes=64)
+        skip_sb = [skip_first[:]] + [skip_rest[:, b, :] for b in range(ROW_TILES - 1)]
         up = [keep.tile([P, U], F32, name=f"up{b}", align_bytes=64) for b in range(ROW_TILES)]
         w2_codes = keep.tile([P, 2, 2, N], U32, align_bytes=64)
         w2_plane = keep.tile([P, 2, N], U8, align_bytes=64)
@@ -60,22 +57,22 @@ def tile_picked_unet_none_p_kernel(
 
         nc.vector.memset(xs_table[:].bitcast(I32), 0)
         nc.vector.memset(up[0][:], 0.0)
-        for b in range(1, ROW_TILES):
-            nc.scalar.copy(out=up[b][:], in_=up[0][:])
         nc.vector.memset(w2_codes[:].bitcast(I32), 0)
         nc.vector.memset(w2_plane[:].bitcast(I32), 0)
+        for b in range(1, ROW_TILES):
+            nc.gpsimd.memset(up[b][:], 0.0)
         make_identity(nc, ident[:])
 
         w1_rows = w1.rearrange("(g p j) c -> g p j c", g=K_PASSES, j=PACK)
         x_rows = x_words.rearrange("g p n t -> g p (n t)").bitcast(I32)
         xs_rows = x_scales.bitcast(I32)
 
-        def load_w1(b):
+        def load_w1(n):
             for g in range(K_PASSES):
-                nc.sync.dma_start(out=w1_raw[b][g][:], in_=w1_rows[g, :, :, b * P : (b + 1) * P])
+                nc.sync.dma_start(out=w1_raw[n][g][:], in_=w1_rows[g, :, :, n * P : n * P + widths[n]])
 
-        nc.sync.dma_start(out=x_table[0][:].bitcast(I32), in_=x_rows[0])
         nc.sync.dma_start(offs_sb[:], offs)
+        nc.sync.dma_start(out=x_table[0][:].bitcast(I32), in_=x_rows[0])
         for q in range(4):
             nc.sync.dma_start(
                 out=xs_table[32 * q : 32 * q + 4 * K_PASSES, :].bitcast(I32), in_=xs_rows[:, 4 * q : 4 * q + 4, :]
@@ -84,11 +81,9 @@ def tile_picked_unet_none_p_kernel(
         nc.sync.dma_start(out=x_table[1][:].bitcast(I32), in_=x_rows[1])
         nc.sync.dma_start(cell_sb[:], cell)
         load_w1(1)
-        for b in range(ROW_TILES):
-            nc.sync.dma_start(out=skip_sb[b][:], in_=skip[b * P : (b + 1) * P, :])
-            if b == 0:
-                load_w1(2)
-                load_w1(3)
+        load_w1(2)
+        nc.sync.dma_start(out=skip_first[:], in_=skip[:P, :])
+        nc.sync.dma_start(out=skip_rest[:], in_=skip[P:, :].rearrange("(b p) v -> p b v", p=P))
         w2_rows = w2_words[0].rearrange("(s p) n t -> p s (n t)", s=2).bitcast(I32)
         for side in range(2):
             nc.sync.dma_start(out=w2_codes[64 * side : 64 * side + 64, side, :, :].bitcast(I32), in_=w2_rows)
@@ -99,167 +94,172 @@ def tile_picked_unet_none_p_kernel(
         def list_part(tile, part):
             return tile[:, part.start // 16 : part.stop // 16]
 
-        def quantise_w1(b):
-            grouped = keep.tile([P, K_PASSES * P * PACK], BF16, name=f"w1_bf{b}", align_bytes=64)
-            for g in range(K_PASSES):
-                nc.scalar.copy(
-                    out=grouped[:, g * P * PACK : (g + 1) * P * PACK].rearrange("p (c i j) -> p c j i", i=4, j=PACK),
-                    in_=w1_raw[b][g][:].rearrange("p j (c i) -> p c j i", i=4),
-                )
-            codes = keep.tile([P, K_PASSES * P], U32, name=f"w1_codes{b}", align_bytes=64)
-            plane = keep.tile([P, K_PASSES * P], U8, name=f"w1_plane{b}", align_bytes=64)
-            nc.vector.quantize_mx(out=codes[:].bitcast(FP8X4), scales=plane[:], in_=grouped[:])
-            return codes, plane
-
-        def first_product(w1_q, part, tag):
-            codes, plane = w1_q
-            acc = psum.tile([P, part.stop - part.start], F32, name="h_acc", tag=tag)
-            edges = [part.start] + ([HALF] if part.start == P else []) + [part.stop]
-            for lo, hi in zip(edges, edges[1:]):
-                for g in range(K_PASSES):
-                    nc.tensor.matmul_mx(
-                        out=acc[:, lo - part.start : hi - part.start],
-                        lhsT=codes[:, g * P : (g + 1) * P].bitcast(FP8X4),
-                        lhsT_scale=plane[:, g * P : (g + 1) * P],
-                        rhs=x_picked[g][:, lo:hi].bitcast(FP8X4),
-                        rhs_scale=xs_picked[4 * g : P, lo:hi],
-                        start=(g == 0),
-                        stop=(g == K_PASSES - 1),
+        def quantise_w1(n, movers, groups):
+            width = widths[n]
+            codes = keep.tile([P, K_PASSES * width], U32, name=f"w1_codes{n}", align_bytes=64)
+            plane = keep.tile([P, K_PASSES * width], U8, name=f"w1_plane{n}", align_bytes=64)
+            for passes in groups:
+                grouped = keep.tile([P, len(passes) * width * PACK], BF16, name="w1_bf", align_bytes=64)
+                for at, g in enumerate(passes):
+                    movers[g](
+                        out=grouped[:, at * width * PACK : (at + 1) * width * PACK].rearrange(
+                            "p (c i j) -> p c j i", i=4, j=PACK
+                        ),
+                        in_=w1_raw[n][g][:].rearrange("p j (c i) -> p c j i", i=4),
                     )
-            return acc
+                cols = slice(passes[0] * width, (passes[-1] + 1) * width)
+                nc.vector.quantize_mx(out=codes[:, cols].bitcast(FP8X4), scales=plane[:, cols], in_=grouped[:])
+            return codes, plane, width
 
-        def leave_psum(acc, h, mover=nc.scalar.copy):
-            mover(out=h[:], in_=acc[:])
-            return h
+        def first_product(w1_q, at, part, acc, passes=range(K_PASSES)):
+            codes, plane, width = w1_q
+            for g in passes:
+                cols = slice(g * width + at, g * width + at + P)
+                nc.tensor.matmul_mx(
+                    out=acc,
+                    lhsT=codes[:, cols].bitcast(FP8X4),
+                    lhsT_scale=plane[:, cols],
+                    rhs=x_picked[g][:, part].bitcast(FP8X4),
+                    rhs_scale=xs_picked[4 * g : P, part],
+                    start=(g == 0),
+                    stop=(g == K_PASSES - 1),
+                )
 
-        def h_tile(part, tag):
-            return keep.tile([P, part.stop - part.start], F32, name="h", tag=tag, align_bytes=64)
+        def scatter_vector(b, part, h):
+            nc.vector.tensor_copy(up[b][:].indirect(list_part(cell_sb, part)), h)
 
-        def scatter(b, part, h):
-            nc.vector.tensor_copy(up[b][:].indirect(list_part(cell_sb, part)), h[:])
-
-        z_turned = []
+        def scatter_scalar(b, part, h):
+            nc.scalar.activation(up[b][:].indirect(list_part(cell_sb, part)), h, COPY)
 
         def turn(banks, source, first):
-            for bank, blocks in banks:
-                for n, j in enumerate(blocks):
+            for jp, bank in enumerate(banks):
+                for n in range(2):
                     for side in range(2):
-                        col = side * SIDE + j * P
+                        col = side * SIDE + jp * PAIR + n * P
                         nc.tensor.matmul(
                             out=bank[:, n, side, :],
                             lhsT=source[:, col : col + P],
                             rhs=ident[:],
                             is_transpose=True,
                             start=(first and n == 0 and side == 0),
-                            stop=(not first and n == len(blocks) - 1 and side == 1),
+                            stop=(not first and n == 1 and side == 1),
                         )
 
         def turn_skip(b, tags):
-            per_bank = 4 // len(tags)
-            banks = [
-                (psum.tile([P, per_bank, 2, P], F32, name="z_bank", tag=tag), range(n * per_bank, (n + 1) * per_bank))
-                for n, tag in enumerate(tags)
-            ]
+            banks = [psum.tile([P, 2, 2, P], F32, name="z_bank", tag=tag) for tag in tags]
             turn(banks, skip_sb[b], True)
             return banks
 
-        def add_up(b, banks, movers):
-            turn(banks, up[b], False)
-            for bank, blocks in banks:
-                for n, j in enumerate(blocks):
-                    movers[j % 2](
-                        out=z_turned[b // 2][j].rearrange("q (u s f a e) -> q f s u a e", u=2, s=2, f=2, e=2)[:, b % 2],
-                        in_=bank[:, n].rearrange("q s (a u e) -> q s u a e", u=2, e=2),
-                    )
+        z_turned = [
+            [keep.tile([P, 2 * PACK * P], BF16, name=f"z_turned{s}_{jp}", align_bytes=64) for jp in range(2)] for s in range(2)
+        ]
 
-        def turn_back(s, per_tile, tags):
-            grouped = [
-                keep.tile([P, per_tile * P * PACK], BF16, name=f"z_bf{s}_{j}", align_bytes=64) for j in range(0, 4, per_tile)
-            ]
-            for j in range(4):
-                bank = psum.tile([P, 2, P], F32, name="back_bank", tag=tags[j // 2])
-                words = z_turned[s][j].bitcast(F32)
-                for u in range(2):
-                    nc.tensor.transpose(bank[:, u, :], words[:, u * P : (u + 1) * P], ident[:])
-                at = (j % per_tile) * 2 * P
-                nc.scalar.copy(
-                    out=grouped[j // per_tile][:].bitcast(F32)[:, at : at + 2 * P].rearrange("p (q u) -> p q u", u=2),
-                    in_=bank[:].rearrange("p u q -> p q u"),
+        def round_z(b, banks, movers):
+            for jp, bank in enumerate(banks):
+                movers[jp](
+                    out=z_turned[b // 2][jp][:].rearrange("q (u m f a e) -> q f m u a e", u=2, m=4, f=2, e=2)[:, b % 2],
+                    in_=bank[:].rearrange("q n s (a u e) -> q (n s) u a e", u=2, e=2),
                 )
+
+        def turn_back(s, tags, movers):
+            grouped = []
+            for jp in range(2):
+                bank = psum.tile([P, 2, 2, P], F32, name="back_bank", tag=tags[jp])
+                words = z_turned[s][jp][:].bitcast(F32)
+                for n in range(2):
+                    for u in range(2):
+                        at = u * PAIR + n * P
+                        nc.tensor.transpose(bank[:, n, u, :], words[:, at : at + P], ident[:])
+                z_bf = keep.tile([P, PAIR * PACK], BF16, name=f"z_bf{s}_{jp}", align_bytes=64)
+                movers[jp](
+                    out=z_bf[:].bitcast(F32).rearrange("p (n q u) -> p n q u", n=2, u=2),
+                    in_=bank[:].rearrange("p n u q -> p n q u"),
+                )
+                grouped.append(z_bf)
             return grouped
 
-        def quantise_z(s, grouped):
-            codes = keep.tile([P, SIDE], U32, name=f"z_codes{s}", align_bytes=64)
-            plane = keep.tile([P, SIDE], U8, name=f"z_plane{s}", align_bytes=64)
-            width = SIDE // len(grouped)
-            parts = [slice(lo, lo + width) for lo in range(0, SIDE, width)]
-            for cols, z_bf in zip(parts, grouped):
-                nc.vector.quantize_mx(out=codes[:, cols].bitcast(FP8X4), scales=plane[:, cols], in_=z_bf[:])
+        def quantise_z(s, jp, z_bf):
+            codes = keep.tile([P, PAIR], U32, name=f"z_codes{s}_{jp}", align_bytes=64)
+            plane = keep.tile([P, PAIR], U8, name=f"z_plane{s}_{jp}", align_bytes=64)
+            nc.vector.quantize_mx(out=codes[:].bitcast(FP8X4), scales=plane[:], in_=z_bf[:])
             return codes, plane
 
-        def second_product(s, z_q, cols, side, acc, start, stop):
+        def second_product(s, z_q, side, acc):
             codes, plane = z_q
             nc.tensor.matmul_mx(
-                out=acc,
+                out=acc[:],
                 lhsT=w2_codes[:, side, s, :].bitcast(FP8X4),
                 lhsT_scale=w2_plane[:, s, :],
-                rhs=codes[:, cols].bitcast(FP8X4),
-                rhs_scale=plane[:, cols],
-                start=start,
-                stop=stop,
+                rhs=codes[:].bitcast(FP8X4),
+                rhs_scale=plane[:],
+                start=(s == 0),
+                stop=(s == 1),
             )
 
-        nc.vector.tensor_copy(x_picked[0][:], x_table[0][:].indirect(offs_sb[:]))
-        nc.vector.tensor_copy(xs_picked[:], xs_table[:].indirect(offs_sb[:]))
-        w1_q = quantise_w1(0)
-        for part in (slice(0, HALF), slice(HALF, S)):
-            nc.vector.tensor_copy(x_picked[1][:, part], x_table[1][:].indirect(list_part(offs_sb, part)))
-
-        on_scalar = (nc.scalar.copy, nc.scalar.copy)
-        last = ROW_TILES - 1
-
-        short, rest = slice(0, P), slice(P, S)
+        on_s, on_v = nc.scalar.copy, nc.vector.tensor_copy
         halves = slice(0, HALF), slice(HALF, S)
         whole = slice(0, S)
 
-        accs = [first_product(w1_q, part, "a") for part in (short, rest)]
-        scatter(0, short, leave_psum(accs[0], h_tile(short, "h0"), nc.vector.tensor_copy))
-        w1_q = quantise_w1(1)
-        scatter(0, rest, leave_psum(accs[1], h_tile(rest, "w1_raw1_1")))
+        nc.vector.tensor_copy(xs_picked[:], xs_table[:].indirect(offs_sb[:]))
+        nc.vector.tensor_copy(x_picked[0][:], x_table[0][:].indirect(offs_sb[:]))
+        w1_q = quantise_w1(0, (on_s, on_s), [(0, 1)])
+        for part in halves:
+            nc.vector.tensor_copy(x_picked[1][:, part], x_table[1][:].indirect(list_part(offs_sb, part)))
 
-        accs = [first_product(w1_q, part, "a") for part in halves]
-        scatter(1, halves[0], leave_psum(accs[0], h_tile(halves[0], "h1")))
-        late_q = [quantise_w1(b) for b in (2, 3)]
-        h_held = shared.tile([P, HALF], F32, name="h_held", offset=0, align_bytes=64)
-        scatter(1, halves[1], leave_psum(accs[1], h_held))
+        accs = [psum.tile([P, HALF], F32, name="h_acc", tag=tag) for tag in ("z2a", "z2b")]
+        for acc, part in zip(accs, halves):
+            first_product(w1_q, 0, part, acc[:])
+        w1_q = quantise_w1(1, (on_s, on_v), [(0, 1)])
+        h0 = keep.tile([P, S], F32, name="h0", tag="w1_raw1_0", align_bytes=64)
+        for acc, part in zip(accs, halves):
+            on_s(out=h0[:, part], in_=acc[:])
+            scatter_scalar(0, part, h0[:, part])
 
-        accs = [first_product(late_q[0], part, "a") for part in (short, rest)]
-        acc_last = first_product(late_q[1], whole, "d")
-        for n, part in enumerate((short, rest)):
-            scatter(2, part, leave_psum(accs[n], h_tile(part, f"h2_{n}")))
-        scatter(last, whole, leave_psum(acc_last, h_tile(whole, "h3")))
+        acc = psum.tile([P, S], F32, name="h_acc", tag="z3a")
+        first_product(w1_q, 0, whole, acc[:])
+        w1_q = quantise_w1(2, (on_v, on_v), [(0,), (1,)])
+        h1 = keep.tile([P, S], F32, name="h1", tag="w1_raw2_1", align_bytes=64)
+        on_v(out=h1[:], in_=acc[:])
+        scatter_vector(1, whole, h1[:])
 
-        z_low = shared.tile([P, 4 * PACK * P], BF16, name="z_low", offset=HALF * 4, align_bytes=64)
-        z_turned.append([z_low[:, j * PACK * P : (j + 1) * PACK * P] for j in range(4)])
-        z_turned.append([keep.tile([P, PACK * P], BF16, name=f"z_high{j}", align_bytes=64)[:] for j in range(4)])
-        add_up(0, turn_skip(0, "bb"), on_scalar)
-        add_up(1, turn_skip(1, "cc"), on_scalar)
-        low_rows = turn_back(0, 4, "dd")
-        banks = [turn_skip(2, "bb"), turn_skip(last, "aacc")]
-        add_up(2, banks[0], on_scalar)
-        low_q = quantise_z(0, low_rows)
-        add_up(last, banks[1], (nc.scalar.copy, nc.vector.tensor_copy))
-        high_q = quantise_z(1, turn_back(1, 1, "db"))
-        for jp in range(2):
-            accs = [psum.tile([P, PAIR], F32, name="out_acc", tag="db"[jp]) for side in range(2)]
-            for side in range(2):
-                second_product(0, low_q, slice(jp * PAIR, (jp + 1) * PAIR), side, accs[side][:], True, False)
+        late = [psum.tile([P, 2, HALF], F32, name="h_acc", tag=tag) for tag in ("z1a", "z1b")]
+        for g in range(K_PASSES):
             for n in range(2):
-                for side in range(2):
-                    lo = jp * PAIR + n * P
-                    second_product(1, high_q, slice(lo, lo + P), side, accs[side][:, n * P : (n + 1) * P], False, n == 1)
-            for side, mover in enumerate((nc.scalar.copy, nc.vector.tensor_copy)):
+                first_product(w1_q, n * P, halves[0], late[n][:, 0, :], (g,))
+        for n in range(2):
+            first_product(w1_q, n * P, halves[1], late[n][:, 1, :])
+        h_late = [keep.tile([P, S], F32, name=f"h_late{n}", align_bytes=64) for n in range(2)]
+        for n in range(2):
+            on_s(out=h_late[n][:], in_=late[n][:].rearrange("p a s -> p (a s)"))
+        scatter_scalar(2, slice(0, SHARE), h_late[0][:, :SHARE])
+        scatter_vector(2, slice(SHARE, S), h_late[0][:, SHARE:])
+        for part in halves:
+            scatter_scalar(3, part, h_late[1][:, part])
+
+        banks = {0: turn_skip(0, ("z0a", "z0b"))}
+        turn(banks[0], up[0], False)
+        banks[1] = turn_skip(1, ("z1a", "z1b"))
+        banks[2] = turn_skip(2, ("z2a", "z2b"))
+        turn(banks[1], up[1], False)
+        banks[3] = turn_skip(3, ("z3a", "z3b"))
+        turn(banks[2], up[2], False)
+        turn(banks[3], up[3], False)
+        round_z(0, banks[0], (on_s, on_s))
+        round_z(1, banks[1], (on_v, on_v))
+        low_rows = turn_back(0, ("z0a", "z0b"), (on_s, on_v))
+        round_z(2, banks[2], (on_s, on_v))
+        round_z(3, banks[3], (on_s, on_v))
+        low_q = [quantise_z(0, jp, low_rows[jp]) for jp in range(2)]
+        high_rows = turn_back(1, ("z1a", "z1b"), (on_s, on_s))
+        accs = [[psum.tile([P, PAIR], F32, name="out_acc", tag=tag) for tag in tags] for tags in (("z2a", "z3a"), ("z2b", "z3b"))]
+        for jp in range(2):
+            for side in range(2):
+                second_product(0, low_q[jp], side, accs[jp][side])
+        for jp in range(2):
+            high_q = quantise_z(1, jp, high_rows[jp])
+            for side, mover in enumerate((on_s, on_v)):
+                second_product(1, high_q, side, accs[jp][side])
                 result = keep.tile([P, PAIR], F32, name=f"result{side}_{jp}")
-                mover(out=result[:], in_=accs[side][:])
+                mover(out=result[:], in_=accs[jp][side][:])
                 lo = side * SIDE + jp * PAIR
                 nc.sync.dma_start(out=out[:, lo : lo + PAIR], in_=result[:])

@@ -23,7 +23,7 @@ HALF = S // 2
 LIST_COLS = S // 16
 SIDE = U // 2
 PAIR = 2 * P
-SHARE = 128
+W1_VECTOR = 320
 
 
 def tile_picked_unet_none_p_kernel(
@@ -42,11 +42,14 @@ def tile_picked_unet_none_p_kernel(
         xs_table = keep.tile([P, T], U8, align_bytes=64)
         x_picked = [keep.tile([P, S], U32, name=f"x_picked{g}", align_bytes=64) for g in range(K_PASSES)]
         xs_picked = keep.tile([P, S], U8, align_bytes=64)
-        widths = (P, P, PAIR)
-        w1_raw = [
-            [keep.tile([P, PACK, w], F32, name=f"w1_raw{n}_{g}", tag=f"w1_raw{n}_{g}", align_bytes=64) for g in range(K_PASSES)]
-            for n, w in enumerate(widths)
+        pieces = slice(0, P), slice(P, PAIR), slice(PAIR, H)
+        w1_first = keep.tile([P, PACK, H], F32, align_bytes=64)
+        w1_second = [
+            keep.tile([P, PACK, cols.stop - cols.start], F32, name=f"w1_second{n}", tag=f"w1_second{n}", align_bytes=64)
+            for n, cols in enumerate(pieces)
         ]
+        w1_codes = [keep.tile([P, H], U32, name=f"w1_codes{g}", align_bytes=64) for g in range(K_PASSES)]
+        w1_plane = [keep.tile([P, H], U8, name=f"w1_plane{g}", align_bytes=64) for g in range(K_PASSES)]
         skip_first = keep.tile([P, U], F32, align_bytes=64)
         skip_rest = keep.tile([P, ROW_TILES - 1, U], F32, align_bytes=64)
         skip_sb = [skip_first[:]] + [skip_rest[:, b, :] for b in range(ROW_TILES - 1)]
@@ -68,15 +71,15 @@ def tile_picked_unet_none_p_kernel(
         xs_rows = x_scales.bitcast(I32)
 
         def load_w1(n):
-            for g in range(K_PASSES):
-                nc.sync.dma_start(out=w1_raw[n][g][:], in_=w1_rows[g, :, :, n * P : n * P + widths[n]])
+            nc.sync.dma_start(out=w1_second[n][:], in_=w1_rows[1, :, :, pieces[n]])
 
         nc.sync.dma_start(offs_sb[:], offs)
-        nc.sync.dma_start(out=x_table[0][:].bitcast(I32), in_=x_rows[0])
+        nc.sync.dma_start(out=w1_first[:], in_=w1_rows[0])
         for q in range(4):
             nc.sync.dma_start(
                 out=xs_table[32 * q : 32 * q + 4 * K_PASSES, :].bitcast(I32), in_=xs_rows[:, 4 * q : 4 * q + 4, :]
             )
+        nc.sync.dma_start(out=x_table[0][:].bitcast(I32), in_=x_rows[0])
         load_w1(0)
         nc.sync.dma_start(out=x_table[1][:].bitcast(I32), in_=x_rows[1])
         nc.sync.dma_start(cell_sb[:], cell)
@@ -94,31 +97,25 @@ def tile_picked_unet_none_p_kernel(
         def list_part(tile, part):
             return tile[:, part.start // 16 : part.stop // 16]
 
-        def quantise_w1(n, movers, groups):
-            width = widths[n]
-            codes = keep.tile([P, K_PASSES * width], U32, name=f"w1_codes{n}", align_bytes=64)
-            plane = keep.tile([P, K_PASSES * width], U8, name=f"w1_plane{n}", align_bytes=64)
-            for passes in groups:
-                grouped = keep.tile([P, len(passes) * width * PACK], BF16, name="w1_bf", align_bytes=64)
-                for at, g in enumerate(passes):
-                    movers[g](
-                        out=grouped[:, at * width * PACK : (at + 1) * width * PACK].rearrange(
-                            "p (c i j) -> p c j i", i=4, j=PACK
-                        ),
-                        in_=w1_raw[n][g][:].rearrange("p j (c i) -> p c j i", i=4),
-                    )
-                cols = slice(passes[0] * width, (passes[-1] + 1) * width)
-                nc.vector.quantize_mx(out=codes[:, cols].bitcast(FP8X4), scales=plane[:, cols], in_=grouped[:])
-            return codes, plane, width
+        def round_w1(mover, grouped, raw):
+            mover(out=grouped.rearrange("p (c i j) -> p c j i", i=4, j=PACK), in_=raw.rearrange("p j (c i) -> p c j i", i=4))
 
-        def first_product(w1_q, at, part, acc, passes=range(K_PASSES)):
-            codes, plane, width = w1_q
+        def quantise_w1(g, cols, grouped):
+            nc.vector.quantize_mx(out=w1_codes[g][:, cols].bitcast(FP8X4), scales=w1_plane[g][:, cols], in_=grouped[:])
+
+        def second_pass_piece(n, mover):
+            cols = pieces[n]
+            grouped = keep.tile([P, (cols.stop - cols.start) * PACK], BF16, name=f"w1_bf{n}", align_bytes=64)
+            round_w1(mover, grouped[:], w1_second[n][:])
+            quantise_w1(1, cols, grouped)
+
+        def first_product(b, part, acc, passes=range(K_PASSES)):
+            cols = slice(b * P, (b + 1) * P)
             for g in passes:
-                cols = slice(g * width + at, g * width + at + P)
                 nc.tensor.matmul_mx(
                     out=acc,
-                    lhsT=codes[:, cols].bitcast(FP8X4),
-                    lhsT_scale=plane[:, cols],
+                    lhsT=w1_codes[g][:, cols].bitcast(FP8X4),
+                    lhsT_scale=w1_plane[g][:, cols],
                     rhs=x_picked[g][:, part].bitcast(FP8X4),
                     rhs_scale=xs_picked[4 * g : P, part],
                     start=(g == 0),
@@ -200,39 +197,45 @@ def tile_picked_unet_none_p_kernel(
         halves = slice(0, HALF), slice(HALF, S)
         whole = slice(0, S)
 
+        grouped = keep.tile([P, H * PACK], BF16, name="w1_bf", align_bytes=64)
+        round_w1(on_v, grouped[:, : W1_VECTOR * PACK], w1_first[:, :, :W1_VECTOR])
+        round_w1(on_s, grouped[:, W1_VECTOR * PACK :], w1_first[:, :, W1_VECTOR:])
+        quantise_w1(0, slice(0, H), grouped)
         nc.vector.tensor_copy(xs_picked[:], xs_table[:].indirect(offs_sb[:]))
-        nc.vector.tensor_copy(x_picked[0][:], x_table[0][:].indirect(offs_sb[:]))
-        w1_q = quantise_w1(0, (on_s, on_s), [(0, 1)])
+        for part in halves:
+            nc.vector.tensor_copy(x_picked[0][:, part], x_table[0][:].indirect(list_part(offs_sb, part)))
+        second_pass_piece(0, on_s)
         for part in halves:
             nc.vector.tensor_copy(x_picked[1][:, part], x_table[1][:].indirect(list_part(offs_sb, part)))
 
         accs = [psum.tile([P, HALF], F32, name="h_acc", tag=tag) for tag in ("z2a", "z2b")]
+        acc1 = psum.tile([P, S], F32, name="h_acc", tag="z3a")
+        late = [psum.tile([P, S], F32, name="h_acc", tag=tag) for tag in ("z1a", "z1b")]
         for acc, part in zip(accs, halves):
-            first_product(w1_q, 0, part, acc[:])
-        w1_q = quantise_w1(1, (on_s, on_v), [(0, 1)])
-        h0 = keep.tile([P, S], F32, name="h0", tag="w1_raw1_0", align_bytes=64)
+            first_product(0, part, acc[:], (0,))
+        first_product(1, whole, acc1[:], (0,))
+        for n in range(2):
+            first_product(2 + n, whole, late[n][:], (0,))
+        for acc, part in zip(accs, halves):
+            first_product(0, part, acc[:], (1,))
+        second_pass_piece(1, on_s)
+        h0 = keep.tile([P, S], F32, name="h0", tag="w1_second1", align_bytes=64)
         for acc, part in zip(accs, halves):
             on_s(out=h0[:, part], in_=acc[:])
             scatter_scalar(0, part, h0[:, part])
 
-        acc = psum.tile([P, S], F32, name="h_acc", tag="z3a")
-        first_product(w1_q, 0, whole, acc[:])
-        w1_q = quantise_w1(2, (on_v, on_v), [(0,), (1,)])
-        h1 = keep.tile([P, S], F32, name="h1", tag="w1_raw2_1", align_bytes=64)
-        on_v(out=h1[:], in_=acc[:])
+        first_product(1, whole, acc1[:], (1,))
+        second_pass_piece(2, on_v)
+        h1 = keep.tile([P, S], F32, name="h1", tag="w1_second2", align_bytes=64)
+        on_v(out=h1[:], in_=acc1[:])
         scatter_vector(1, whole, h1[:])
 
-        late = [psum.tile([P, 2, HALF], F32, name="h_acc", tag=tag) for tag in ("z1a", "z1b")]
-        for g in range(K_PASSES):
-            for n in range(2):
-                first_product(w1_q, n * P, halves[0], late[n][:, 0, :], (g,))
         for n in range(2):
-            first_product(w1_q, n * P, halves[1], late[n][:, 1, :])
+            first_product(2 + n, whole, late[n][:], (1,))
         h_late = [keep.tile([P, S], F32, name=f"h_late{n}", align_bytes=64) for n in range(2)]
         for n in range(2):
-            on_s(out=h_late[n][:], in_=late[n][:].rearrange("p a s -> p (a s)"))
-        scatter_scalar(2, slice(0, SHARE), h_late[0][:, :SHARE])
-        scatter_vector(2, slice(SHARE, S), h_late[0][:, SHARE:])
+            on_s(out=h_late[n][:], in_=late[n][:])
+        scatter_vector(2, whole, h_late[0][:])
         for part in halves:
             scatter_scalar(3, part, h_late[1][:, part])
 

@@ -54,13 +54,12 @@ def tile_picked_unet_none_p_kernel(
         skip_rest = keep.tile([P, ROW_TILES - 1, U], F32, align_bytes=64)
         skip_sb = [skip_first[:]] + [skip_rest[:, b, :] for b in range(ROW_TILES - 1)]
         up = [keep.tile([P, U], F32, name=f"up{b}", align_bytes=64) for b in range(ROW_TILES)]
-        w2_codes = keep.tile([P, 2, 2, N], U32, align_bytes=64)
-        w2_plane = keep.tile([P, 2, N], U8, align_bytes=64)
+        w2_codes = keep.tile([P, N], U32, align_bytes=64)
+        w2_plane = keep.tile([P, N], U8, align_bytes=64)
         ident = keep.tile([P, P], F32, align_bytes=64)
 
         nc.vector.memset(xs_table[:].bitcast(I32), 0)
         nc.vector.memset(up[0][:], 0.0)
-        nc.vector.memset(w2_codes[:].bitcast(I32), 0)
         nc.vector.memset(w2_plane[:].bitcast(I32), 0)
         for b in range(1, ROW_TILES):
             nc.gpsimd.memset(up[b][:], 0.0)
@@ -87,12 +86,11 @@ def tile_picked_unet_none_p_kernel(
         load_w1(2)
         nc.sync.dma_start(out=skip_first[:], in_=skip[:P, :])
         nc.sync.dma_start(out=skip_rest[:], in_=skip[P:, :].rearrange("(b p) v -> p b v", p=P))
-        w2_rows = w2_words[0].rearrange("(s p) n t -> p s (n t)", s=2).bitcast(I32)
-        for side in range(2):
-            nc.sync.dma_start(out=w2_codes[64 * side : 64 * side + 64, side, :, :].bitcast(I32), in_=w2_rows)
-        w2s_rows = w2_scales[0].rearrange("(s a r) n -> a r s n", s=2, a=2).bitcast(I32)
+        nc.sync.dma_start(out=w2_codes[:].bitcast(I32), in_=w2_words[0].rearrange("p n t -> p (n t)").bitcast(I32))
         for q in range(4):
-            nc.sync.dma_start(out=w2_plane[32 * q : 32 * q + 4, :, :].bitcast(I32), in_=w2s_rows[q % 2])
+            nc.sync.dma_start(
+                out=w2_plane[32 * q : 32 * q + 4, :].bitcast(I32), in_=w2_scales[0, 4 * q : 4 * q + 4, :].bitcast(I32)
+            )
 
         def list_part(tile, part):
             return tile[:, part.start // 16 : part.stop // 16]
@@ -128,70 +126,61 @@ def tile_picked_unet_none_p_kernel(
         def scatter_scalar(b, part, h):
             nc.scalar.activation(up[b][:].indirect(list_part(cell_sb, part)), h, COPY)
 
-        def turn(banks, source, first):
-            for jp, bank in enumerate(banks):
-                for n in range(2):
-                    for side in range(2):
-                        col = side * SIDE + jp * PAIR + n * P
-                        nc.tensor.matmul(
-                            out=bank[:, n, side, :],
-                            lhsT=source[:, col : col + P],
-                            rhs=ident[:],
-                            is_transpose=True,
-                            start=(first and n == 0 and side == 0),
-                            stop=(not first and n == 1 and side == 1),
-                        )
-
-        def turn_skip(b, tags):
-            banks = [psum.tile([P, 2, 2, P], F32, name="z_bank", tag=tag) for tag in tags]
-            turn(banks, skip_sb[b], True)
-            return banks
-
-        z_turned = [
-            [keep.tile([P, 2 * PACK * P], BF16, name=f"z_turned{s}_{jp}", align_bytes=64) for jp in range(2)] for s in range(2)
-        ]
-
-        def round_z(b, banks, movers):
-            for jp, bank in enumerate(banks):
-                movers[jp](
-                    out=z_turned[b // 2][jp][:].rearrange("q (u m f a e) -> q f m u a e", u=2, m=4, f=2, e=2)[:, b % 2],
-                    in_=bank[:].rearrange("q n s (a u e) -> q (n s) u a e", u=2, e=2),
+        def turn(b, side, source, first):
+            for m in range(4):
+                col = side * SIDE + m * P
+                nc.tensor.matmul(
+                    out=banks[b][side][:, m, :],
+                    lhsT=source[:, col : col + P],
+                    rhs=ident[:],
+                    is_transpose=True,
+                    start=(first and m == 0),
+                    stop=(not first and m == 3),
                 )
 
-        def turn_back(s, tags, movers):
-            grouped = []
-            for jp in range(2):
-                bank = psum.tile([P, 2, 2, P], F32, name="back_bank", tag=tags[jp])
-                words = z_turned[s][jp][:].bitcast(F32)
-                for n in range(2):
-                    for u in range(2):
-                        at = u * PAIR + n * P
-                        nc.tensor.transpose(bank[:, n, u, :], words[:, at : at + P], ident[:])
-                z_bf = keep.tile([P, PAIR * PACK], BF16, name=f"z_bf{s}_{jp}", align_bytes=64)
-                movers[jp](
-                    out=z_bf[:].bitcast(F32).rearrange("p (n q u) -> p n q u", n=2, u=2),
-                    in_=bank[:].rearrange("p n u q -> p n q u"),
-                )
-                grouped.append(z_bf)
-            return grouped
+        def turn_skip(b):
+            for side in range(2):
+                turn(b, side, skip_sb[b], True)
 
-        def quantise_z(s, jp, z_bf):
-            codes = keep.tile([P, PAIR], U32, name=f"z_codes{s}_{jp}", align_bytes=64)
-            plane = keep.tile([P, PAIR], U8, name=f"z_plane{s}_{jp}", align_bytes=64)
+        z_turned = [keep.tile([P, 4 * H], BF16, name=f"z_turned{side}", align_bytes=64) for side in range(2)]
+
+        def round_z(b, side, mover):
+            mover(
+                out=z_turned[side][:].rearrange("q (m u b a e) -> q b m u a e", m=4, u=2, b=ROW_TILES, e=2)[:, b],
+                in_=banks[b][side][:].rearrange("q m (a u e) -> q m u a e", u=2, e=2),
+            )
+
+        def turn_back(block, tag, mover):
+            bank = psum.tile([P, 2, 2, P], F32, name="back_bank", tag=tag)
+            words = z_turned[block // 2][:].bitcast(F32)
+            for n in range(2):
+                for u in range(2):
+                    lo = ((block % 2) * 2 + n) * PAIR + u * P
+                    nc.tensor.transpose(bank[:, n, u, :], words[:, lo : lo + P], ident[:])
+            z_bf = keep.tile([P, PAIR * PACK], BF16, name=f"z_bf{block}", align_bytes=64)
+            mover(
+                out=z_bf[:].bitcast(F32).rearrange("p (n q u) -> p n q u", n=2, u=2),
+                in_=bank[:].rearrange("p n u q -> p n q u"),
+            )
+            return z_bf
+
+        def second_product(block, z_bf, tag, mover):
+            codes = keep.tile([P, PAIR], U32, name=f"z_codes{block}", align_bytes=64)
+            plane = keep.tile([P, PAIR], U8, name=f"z_plane{block}", align_bytes=64)
             nc.vector.quantize_mx(out=codes[:].bitcast(FP8X4), scales=plane[:], in_=z_bf[:])
-            return codes, plane
-
-        def second_product(s, z_q, side, acc):
-            codes, plane = z_q
+            acc = psum.tile([P, PAIR], F32, name="out_acc", tag=tag)
             nc.tensor.matmul_mx(
                 out=acc[:],
-                lhsT=w2_codes[:, side, s, :].bitcast(FP8X4),
-                lhsT_scale=w2_plane[:, s, :],
+                lhsT=w2_codes[:].bitcast(FP8X4),
+                lhsT_scale=w2_plane[:],
                 rhs=codes[:].bitcast(FP8X4),
                 rhs_scale=plane[:],
-                start=(s == 0),
-                stop=(s == 1),
+                start=True,
+                stop=True,
             )
+            result = keep.tile([P, PAIR], F32, name=f"result{block}")
+            mover(out=result[:], in_=acc[:])
+            nc.sync.dma_start(out=out[:, block * PAIR : (block + 1) * PAIR], in_=result[:])
 
         on_s, on_v = nc.scalar.copy, nc.vector.tensor_copy
         halves = slice(0, HALF), slice(HALF, S)
@@ -210,12 +199,14 @@ def tile_picked_unet_none_p_kernel(
 
         accs = [psum.tile([P, HALF], F32, name="h_acc", tag=tag) for tag in ("z2a", "z2b")]
         acc1 = psum.tile([P, S], F32, name="h_acc", tag="z3a")
-        late = [psum.tile([P, S], F32, name="h_acc", tag=tag) for tag in ("z1a", "z1b")]
+        acc2 = psum.tile([P, S], F32, name="h_acc", tag="z1a")
+        accs3 = [psum.tile([P, HALF], F32, name="h_acc", tag=tag) for tag in ("z1b", "z3b")]
         for acc, part in zip(accs, halves):
             first_product(0, part, acc[:], (0,))
         first_product(1, whole, acc1[:], (0,))
-        for n in range(2):
-            first_product(2 + n, whole, late[n][:], (0,))
+        first_product(2, whole, acc2[:], (0,))
+        for acc, part in zip(accs3, halves):
+            first_product(3, part, acc[:], (0,))
         for acc, part in zip(accs, halves):
             first_product(0, part, acc[:], (1,))
         second_pass_piece(1, on_s)
@@ -230,39 +221,33 @@ def tile_picked_unet_none_p_kernel(
         on_v(out=h1[:], in_=acc1[:])
         scatter_vector(1, whole, h1[:])
 
-        for n in range(2):
-            first_product(2 + n, whole, late[n][:], (1,))
-        h_late = [keep.tile([P, S], F32, name=f"h_late{n}", align_bytes=64) for n in range(2)]
-        for n in range(2):
-            on_s(out=h_late[n][:], in_=late[n][:])
-        scatter_vector(2, whole, h_late[0][:])
-        for part in halves:
-            scatter_scalar(3, part, h_late[1][:, part])
+        first_product(3, halves[0], accs3[0][:], (1,))
+        first_product(2, whole, acc2[:], (1,))
+        first_product(3, halves[1], accs3[1][:], (1,))
+        h2, h3 = (keep.tile([P, S], F32, name=f"h{b}", align_bytes=64) for b in (2, 3))
+        on_s(out=h3[:, halves[0]], in_=accs3[0][:])
+        on_s(out=h2[:], in_=acc2[:])
+        scatter_vector(2, whole, h2[:])
+        scatter_scalar(3, halves[0], h3[:, halves[0]])
+        on_s(out=h3[:, halves[1]], in_=accs3[1][:])
+        scatter_scalar(3, halves[1], h3[:, halves[1]])
 
-        banks = {0: turn_skip(0, ("z0a", "z0b"))}
-        turn(banks[0], up[0], False)
-        banks[1] = turn_skip(1, ("z1a", "z1b"))
-        banks[2] = turn_skip(2, ("z2a", "z2b"))
-        turn(banks[1], up[1], False)
-        banks[3] = turn_skip(3, ("z3a", "z3b"))
-        turn(banks[2], up[2], False)
-        turn(banks[3], up[3], False)
-        round_z(0, banks[0], (on_s, on_s))
-        round_z(1, banks[1], (on_v, on_v))
-        low_rows = turn_back(0, ("z0a", "z0b"), (on_s, on_v))
-        round_z(2, banks[2], (on_s, on_v))
-        round_z(3, banks[3], (on_s, on_v))
-        low_q = [quantise_z(0, jp, low_rows[jp]) for jp in range(2)]
-        high_rows = turn_back(1, ("z1a", "z1b"), (on_s, on_s))
-        accs = [[psum.tile([P, PAIR], F32, name="out_acc", tag=tag) for tag in tags] for tags in (("z2a", "z3a"), ("z2b", "z3b"))]
-        for jp in range(2):
-            for side in range(2):
-                second_product(0, low_q[jp], side, accs[jp][side])
-        for jp in range(2):
-            high_q = quantise_z(1, jp, high_rows[jp])
-            for side, mover in enumerate((on_s, on_v)):
-                second_product(1, high_q, side, accs[jp][side])
-                result = keep.tile([P, PAIR], F32, name=f"result{side}_{jp}")
-                mover(out=result[:], in_=accs[jp][side][:])
-                lo = side * SIDE + jp * PAIR
-                nc.sync.dma_start(out=out[:, lo : lo + PAIR], in_=result[:])
+        banks = [[psum.tile([P, 4, P], F32, name="z_bank", tag=f"z{b}{side}") for side in "ab"] for b in range(ROW_TILES)]
+        turn_skip(0)
+        for side in range(2):
+            turn(0, side, up[0], False)
+        turn_skip(1)
+        turn_skip(2)
+        for side in range(2):
+            turn(1, side, up[1], False)
+        turn_skip(3)
+        for side in range(2):
+            for b in (2, 3):
+                turn(b, side, up[b], False)
+        for b, side, mover in (
+            (0, 0, on_v), (1, 0, on_v), (2, 0, on_s), (3, 0, on_v), (0, 1, on_s), (1, 1, on_s), (2, 1, on_v), (3, 1, on_v),
+        ):
+            round_z(b, side, mover)
+        rows = [turn_back(block, tag, mover) for block, (tag, mover) in enumerate((("z0a", on_s), ("z1a", on_s), ("z0b", on_v), ("z1b", on_s)))]
+        for block, (tag, mover) in enumerate((("z2a", on_s), ("z3a", on_s), ("z2b", on_s), ("z3b", on_v))):
+            second_product(block, rows[block], tag, mover)

@@ -1,7 +1,6 @@
 from contextlib import ExitStack
 
 import concourse.mybir as mybir
-from concourse.masks import make_identity
 
 K, T, S, H, N, U = 1024, 2048, 512, 512, 128, 1024
 FLOPS = 2 * K * H * S + 2 * H * N * U
@@ -14,16 +13,15 @@ U16 = mybir.dt.uint16
 U8 = mybir.dt.uint8
 FP8X4 = mybir.dt.float8_e4m3fn_x4
 COPY = mybir.ActivationFunctionType.Copy
+ADD = mybir.AluOpType.add
 
 P = 128
 PACK = 4
 K_PASSES = K // (P * PACK)
-ROW_TILES = H // P
 HALF = S // 2
 LIST_COLS = S // 16
-SIDE = U // 2
-PAIR = 2 * P
-W1_VECTOR = 320
+UNIT = 128
+W1_VECTOR = 80
 
 
 def tile_picked_unet_none_p_kernel(
@@ -42,212 +40,181 @@ def tile_picked_unet_none_p_kernel(
         xs_table = keep.tile([P, T], U8, align_bytes=64)
         x_picked = [keep.tile([P, S], U32, name=f"x_picked{g}", align_bytes=64) for g in range(K_PASSES)]
         xs_picked = keep.tile([P, S], U8, align_bytes=64)
-        pieces = slice(0, P), slice(P, PAIR), slice(PAIR, H)
-        w1_first = keep.tile([P, PACK, H], F32, align_bytes=64)
-        w1_second = [
-            keep.tile([P, PACK, cols.stop - cols.start], F32, name=f"w1_second{n}", tag=f"w1_second{n}", align_bytes=64)
-            for n, cols in enumerate(pieces)
-        ]
+        w1_raw = [keep.tile([P, PACK, H], F32, name=f"w1_raw{g}", align_bytes=64) for g in range(K_PASSES)]
         w1_codes = [keep.tile([P, H], U32, name=f"w1_codes{g}", align_bytes=64) for g in range(K_PASSES)]
         w1_plane = [keep.tile([P, H], U8, name=f"w1_plane{g}", align_bytes=64) for g in range(K_PASSES)]
         skip_first = keep.tile([P, U], F32, align_bytes=64)
-        skip_rest = keep.tile([P, ROW_TILES - 1, U], F32, align_bytes=64)
-        skip_sb = [skip_first[:]] + [skip_rest[:, b, :] for b in range(ROW_TILES - 1)]
-        up = [keep.tile([P, U], F32, name=f"up{b}", align_bytes=64) for b in range(ROW_TILES)]
+        skip_rest = keep.tile([P, PACK - 1, U], F32, align_bytes=64)
+        skip_sb = [skip_first[:]] + [skip_rest[:, t, :] for t in range(PACK - 1)]
+        up = [keep.tile([P, U], F32, name=f"up{t}", align_bytes=64) for t in range(PACK)]
+        z_planes = keep.tile([P, U // UNIT, PACK, UNIT], BF16, align_bytes=64)
         w2_codes = keep.tile([P, N], U32, align_bytes=64)
         w2_plane = keep.tile([P, N], U8, align_bytes=64)
-        ident = keep.tile([P, P], F32, align_bytes=64)
 
         nc.vector.memset(xs_table[:].bitcast(I32), 0)
         nc.vector.memset(up[0][:], 0.0)
         nc.vector.memset(w2_plane[:].bitcast(I32), 0)
-        for b in range(1, ROW_TILES):
-            nc.gpsimd.memset(up[b][:], 0.0)
-        make_identity(nc, ident[:])
+        for t in range(1, PACK):
+            nc.gpsimd.memset(up[t][:], 0.0)
 
         w1_rows = w1.rearrange("(g p j) c -> g p j c", g=K_PASSES, j=PACK)
         x_rows = x_words.rearrange("g p n t -> g p (n t)").bitcast(I32)
         xs_rows = x_scales.bitcast(I32)
-
-        def load_w1(n):
-            nc.sync.dma_start(out=w1_second[n][:], in_=w1_rows[1, :, :, pieces[n]])
+        skip_rows = skip.rearrange("(p t) v -> p t v", t=PACK)
 
         nc.sync.dma_start(offs_sb[:], offs)
-        nc.sync.dma_start(out=w1_first[:], in_=w1_rows[0])
+        nc.sync.dma_start(out=w1_raw[0][:], in_=w1_rows[0])
         for q in range(4):
             nc.sync.dma_start(
                 out=xs_table[32 * q : 32 * q + 4 * K_PASSES, :].bitcast(I32), in_=xs_rows[:, 4 * q : 4 * q + 4, :]
             )
         nc.sync.dma_start(out=x_table[0][:].bitcast(I32), in_=x_rows[0])
-        load_w1(0)
-        nc.sync.dma_start(out=x_table[1][:].bitcast(I32), in_=x_rows[1])
+        nc.sync.dma_start(out=w1_raw[1][:], in_=w1_rows[1])
         nc.sync.dma_start(cell_sb[:], cell)
-        load_w1(1)
-        load_w1(2)
-        nc.sync.dma_start(out=skip_first[:], in_=skip[:P, :])
-        nc.sync.dma_start(out=skip_rest[:], in_=skip[P:, :].rearrange("(b p) v -> p b v", p=P))
+        nc.sync.dma_start(out=x_table[1][:].bitcast(I32), in_=x_rows[1])
+        nc.sync.dma_start(out=skip_first[:], in_=skip_rows[:, 0, :])
+        nc.sync.dma_start(out=skip_rest[:], in_=skip_rows[:, 1:, :])
         nc.sync.dma_start(out=w2_codes[:].bitcast(I32), in_=w2_words[0].rearrange("p n t -> p (n t)").bitcast(I32))
         for q in range(4):
             nc.sync.dma_start(
                 out=w2_plane[32 * q : 32 * q + 4, :].bitcast(I32), in_=w2_scales[0, 4 * q : 4 * q + 4, :].bitcast(I32)
             )
 
-        def list_part(tile, part):
-            return tile[:, part.start // 16 : part.stop // 16]
-
-        def round_w1(mover, grouped, raw):
-            mover(out=grouped.rearrange("p (c i j) -> p c j i", i=4, j=PACK), in_=raw.rearrange("p j (c i) -> p c j i", i=4))
-
-        def quantise_w1(g, cols, grouped):
-            nc.vector.quantize_mx(out=w1_codes[g][:, cols].bitcast(FP8X4), scales=w1_plane[g][:, cols], in_=grouped[:])
-
-        def second_pass_piece(n, mover):
-            cols = pieces[n]
-            grouped = keep.tile([P, (cols.stop - cols.start) * PACK], BF16, name=f"w1_bf{n}", align_bytes=64)
-            round_w1(mover, grouped[:], w1_second[n][:])
-            quantise_w1(1, cols, grouped)
-
-        def first_product(b, part, acc, passes=range(K_PASSES)):
-            cols = slice(b * P, (b + 1) * P)
-            for g in passes:
-                nc.tensor.matmul_mx(
-                    out=acc,
-                    lhsT=w1_codes[g][:, cols].bitcast(FP8X4),
-                    lhsT_scale=w1_plane[g][:, cols],
-                    rhs=x_picked[g][:, part].bitcast(FP8X4),
-                    rhs_scale=xs_picked[4 * g : P, part],
-                    start=(g == 0),
-                    stop=(g == K_PASSES - 1),
-                )
-
-        def scatter_vector(b, part, h):
-            nc.vector.tensor_copy(up[b][:].indirect(list_part(cell_sb, part)), h)
-
-        def scatter_scalar(b, part, h):
-            nc.scalar.activation(up[b][:].indirect(list_part(cell_sb, part)), h, COPY)
-
-        def turn(b, side, source, first):
-            for m in range(4):
-                col = side * SIDE + m * P
-                nc.tensor.matmul(
-                    out=banks[b][side][:, m, :],
-                    lhsT=source[:, col : col + P],
-                    rhs=ident[:],
-                    is_transpose=True,
-                    start=(first and m == 0),
-                    stop=(not first and m == 3),
-                )
-
-        def turn_skip(b):
-            for side in range(2):
-                turn(b, side, skip_sb[b], True)
-
-        z_turned = [keep.tile([P, 4 * H], BF16, name=f"z_turned{side}", align_bytes=64) for side in range(2)]
-
-        def round_z(b, side, mover):
-            mover(
-                out=z_turned[side][:].rearrange("q (m u b a e) -> q b m u a e", m=4, u=2, b=ROW_TILES, e=2)[:, b],
-                in_=banks[b][side][:].rearrange("q m (a u e) -> q m u a e", u=2, e=2),
-            )
-
-        def turn_back(block, tag, mover):
-            bank = psum.tile([P, 2, 2, P], F32, name="back_bank", tag=tag)
-            words = z_turned[block // 2][:].bitcast(F32)
-            for n in range(2):
-                for u in range(2):
-                    lo = ((block % 2) * 2 + n) * PAIR + u * P
-                    nc.tensor.transpose(bank[:, n, u, :], words[:, lo : lo + P], ident[:])
-            z_bf = keep.tile([P, PAIR * PACK], BF16, name=f"z_bf{block}", align_bytes=64)
-            mover(
-                out=z_bf[:].bitcast(F32).rearrange("p (n q u) -> p n q u", n=2, u=2),
-                in_=bank[:].rearrange("p n u q -> p n q u"),
-            )
-            return z_bf
-
-        def second_product(block, z_bf, tag, mover):
-            codes = keep.tile([P, PAIR], U32, name=f"z_codes{block}", align_bytes=64)
-            plane = keep.tile([P, PAIR], U8, name=f"z_plane{block}", align_bytes=64)
-            nc.vector.quantize_mx(out=codes[:].bitcast(FP8X4), scales=plane[:], in_=z_bf[:])
-            acc = psum.tile([P, PAIR], F32, name="out_acc", tag=tag)
-            nc.tensor.matmul_mx(
-                out=acc[:],
-                lhsT=w2_codes[:].bitcast(FP8X4),
-                lhsT_scale=w2_plane[:],
-                rhs=codes[:].bitcast(FP8X4),
-                rhs_scale=plane[:],
-                start=True,
-                stop=True,
-            )
-            result = keep.tile([P, PAIR], F32, name=f"result{block}")
-            mover(out=result[:], in_=acc[:])
-            nc.sync.dma_start(out=out[:, block * PAIR : (block + 1) * PAIR], in_=result[:])
-
         on_s, on_v = nc.scalar.copy, nc.vector.tensor_copy
         halves = slice(0, HALF), slice(HALF, S)
         whole = slice(0, S)
 
-        grouped = keep.tile([P, H * PACK], BF16, name="w1_bf", align_bytes=64)
-        round_w1(on_v, grouped[:, : W1_VECTOR * PACK], w1_first[:, :, :W1_VECTOR])
-        round_w1(on_s, grouped[:, W1_VECTOR * PACK :], w1_first[:, :, W1_VECTOR:])
-        quantise_w1(0, slice(0, H), grouped)
+        def list_part(tile, part):
+            return tile[:, part.start // 16 : part.stop // 16]
+
+        def quantise_w1(g):
+            grouped = keep.tile([P, H * PACK], BF16, name=f"w1_bf{g}", align_bytes=64)
+            dealt = grouped[:].rearrange("p (t m j) -> p m j t", t=PACK, j=PACK)
+            raw = w1_raw[g][:].rearrange("p j (m t) -> p m j t", t=PACK)
+            on_v(out=dealt[:, :W1_VECTOR], in_=raw[:, :W1_VECTOR])
+            on_s(out=dealt[:, W1_VECTOR:], in_=raw[:, W1_VECTOR:])
+            nc.vector.quantize_mx(out=w1_codes[g][:].bitcast(FP8X4), scales=w1_plane[g][:], in_=grouped[:])
+
+        def gather_words(g, part):
+            nc.vector.tensor_copy(x_picked[g][:, part], x_table[g][:].indirect(list_part(offs_sb, part)))
+
+        def first_product(t, part, acc, g, start, stop):
+            cols = slice(t * P, (t + 1) * P)
+            nc.tensor.matmul_mx(
+                out=acc,
+                lhsT=w1_codes[g][:, cols].bitcast(FP8X4),
+                lhsT_scale=w1_plane[g][:, cols],
+                rhs=x_picked[g][:, part].bitcast(FP8X4),
+                rhs_scale=xs_picked[4 * g : P, part],
+                start=start,
+                stop=stop,
+            )
+
+        def scatter_vector(t, part, h):
+            nc.vector.tensor_copy(up[t][:].indirect(list_part(cell_sb, part)), h[:, part])
+
+        def scatter_scalar(t, part, h):
+            nc.scalar.activation(up[t][:].indirect(list_part(cell_sb, part)), h[:, part], COPY)
+
+        def add_skip(engine, t, cols):
+            engine.tensor_tensor(
+                z_planes[:, cols.start // UNIT : cols.stop // UNIT, t, :],
+                up[t][:, cols].rearrange("p (n v) -> p n v", v=UNIT),
+                skip_sb[t][:, cols].rearrange("p (n v) -> p n v", v=UNIT),
+                ADD,
+            )
+
+        first, second, rest = slice(0, P), slice(P, HALF), slice(P, S)
+        quantise_w1(0)
         nc.vector.tensor_copy(xs_picked[:], xs_table[:].indirect(offs_sb[:]))
+        gather_words(0, whole)
+        quantise_w1(1)
+        for part in (first, second, halves[1]):
+            gather_words(1, part)
+
+        held = [(0, first), (0, rest), (1, whole), (2, whole), (3, whole)]
+        accs = [psum.tile([P, part.stop - part.start], F32, name="h_acc", tag=f"bank{n}") for n, (t, part) in enumerate(held)]
+        steps = [
+            (0, first), (1, second), (2, halves[0]), (3, halves[0]),
+            (1, halves[1]), (2, halves[1]), (3, halves[1]), (4, whole),
+        ]
+        for g in range(K_PASSES):
+            for n, part in steps:
+                t, span = held[n]
+                first_product(
+                    t,
+                    part,
+                    accs[n][:, part.start - span.start : part.stop - span.start],
+                    g,
+                    g == 0 and part.start == span.start,
+                    g == K_PASSES - 1 and part.stop == span.stop,
+                )
+
+        h = [keep.tile([P, S], F32, name=f"h{t}", align_bytes=64) for t in range(PACK)]
+        on_s(out=h[0][:, first], in_=accs[0][:])
+        scatter_scalar(0, first, h[0])
+        on_v(out=h[0][:, rest], in_=accs[1][:])
+        on_s(out=h[1][:], in_=accs[2][:])
+        on_v(out=h[2][:], in_=accs[3][:])
+        on_s(out=h[3][:], in_=accs[4][:])
+        scatter_vector(0, rest, h[0])
+        scatter_vector(2, whole, h[2])
         for part in halves:
-            nc.vector.tensor_copy(x_picked[0][:, part], x_table[0][:].indirect(list_part(offs_sb, part)))
-        second_pass_piece(0, on_s)
-        for part in halves:
-            nc.vector.tensor_copy(x_picked[1][:, part], x_table[1][:].indirect(list_part(offs_sb, part)))
+            for t in (1, 3):
+                scatter_scalar(t, part, h[t])
 
-        accs = [psum.tile([P, HALF], F32, name="h_acc", tag=tag) for tag in ("z2a", "z2b")]
-        acc1 = psum.tile([P, S], F32, name="h_acc", tag="z3a")
-        acc2 = psum.tile([P, S], F32, name="h_acc", tag="z1a")
-        accs3 = [psum.tile([P, HALF], F32, name="h_acc", tag=tag) for tag in ("z1b", "z3b")]
-        for acc, part in zip(accs, halves):
-            first_product(0, part, acc[:], (0,))
-        first_product(1, whole, acc1[:], (0,))
-        first_product(2, whole, acc2[:], (0,))
-        for acc, part in zip(accs3, halves):
-            first_product(3, part, acc[:], (0,))
-        for acc, part in zip(accs, halves):
-            first_product(0, part, acc[:], (1,))
-        second_pass_piece(1, on_s)
-        h0 = keep.tile([P, S], F32, name="h0", tag="w1_second1", align_bytes=64)
-        for acc, part in zip(accs, halves):
-            on_s(out=h0[:, part], in_=acc[:])
-            scatter_scalar(0, part, h0[:, part])
+        def cells(first_unit, units):
+            return slice(first_unit * UNIT, (first_unit + units) * UNIT)
 
-        first_product(1, whole, acc1[:], (1,))
-        second_pass_piece(2, on_v)
-        h1 = keep.tile([P, S], F32, name="h1", tag="w1_second2", align_bytes=64)
-        on_v(out=h1[:], in_=acc1[:])
-        scatter_vector(1, whole, h1[:])
+        z_bf = keep.tile([P, U * PACK], BF16, align_bytes=64)
+        z_codes = keep.tile([P, U], U32, align_bytes=64)
+        z_plane = keep.tile([P, U], U8, align_bytes=64)
 
-        first_product(3, halves[0], accs3[0][:], (1,))
-        first_product(2, whole, acc2[:], (1,))
-        first_product(3, halves[1], accs3[1][:], (1,))
-        h2, h3 = (keep.tile([P, S], F32, name=f"h{b}", align_bytes=64) for b in (2, 3))
-        on_s(out=h3[:, halves[0]], in_=accs3[0][:])
-        on_s(out=h2[:], in_=acc2[:])
-        scatter_vector(2, whole, h2[:])
-        scatter_scalar(3, halves[0], h3[:, halves[0]])
-        on_s(out=h3[:, halves[1]], in_=accs3[1][:])
-        scatter_scalar(3, halves[1], h3[:, halves[1]])
+        def weave(cols, mover):
+            mover(
+                out=z_bf[:, cols.start * PACK : cols.stop * PACK].rearrange("p (n c i t) -> p n c t i", c=UNIT // 4, i=4, t=PACK),
+                in_=z_planes[:, cols.start // UNIT : cols.stop // UNIT].rearrange("p n t (c i) -> p n c t i", i=4),
+            )
 
-        banks = [[psum.tile([P, 4, P], F32, name="z_bank", tag=f"z{b}{side}") for side in "ab"] for b in range(ROW_TILES)]
-        turn_skip(0)
-        for side in range(2):
-            turn(0, side, up[0], False)
-        turn_skip(1)
-        turn_skip(2)
-        for side in range(2):
-            turn(1, side, up[1], False)
-        turn_skip(3)
-        for side in range(2):
-            for b in (2, 3):
-                turn(b, side, up[b], False)
-        for b, side, mover in (
-            (0, 0, on_v), (1, 0, on_v), (2, 0, on_s), (3, 0, on_v), (0, 1, on_s), (1, 1, on_s), (2, 1, on_v), (3, 1, on_v),
+        def quantise_z(cols):
+            nc.vector.quantize_mx(
+                out=z_codes[:, cols].bitcast(FP8X4), scales=z_plane[:, cols], in_=z_bf[:, cols.start * PACK : cols.stop * PACK]
+            )
+
+        def second_product(cols, bank, mover):
+            width = cols.stop - cols.start
+            acc = psum.tile([P, width], F32, name="out_acc", tag=f"bank{bank}")
+            nc.tensor.matmul_mx(
+                out=acc[:],
+                lhsT=w2_codes[:].bitcast(FP8X4),
+                lhsT_scale=w2_plane[:],
+                rhs=z_codes[:, cols].bitcast(FP8X4),
+                rhs_scale=z_plane[:, cols],
+                start=True,
+                stop=True,
+            )
+            result = keep.tile([P, width], F32, name=f"result{cols.start}")
+            mover(out=result[:], in_=acc[:])
+            nc.sync.dma_start(out=out[:, cols], in_=result[:])
+
+        low, high = cells(0, 4), cells(4, 4)
+        add_skip(nc.gpsimd, 0, cells(0, 8))
+        for t in (2, 1):
+            add_skip(nc.vector, t, low)
+        add_skip(nc.vector, 3, cells(0, 1))
+        weave(cells(0, 1), on_s)
+        add_skip(nc.vector, 3, cells(1, 3))
+        weave(cells(1, 1), on_s)
+        weave(cells(2, 2), on_s)
+        for t in (2, 1, 3):
+            add_skip(nc.vector, t, high)
+        weave(cells(6, 1), on_s)
+        weave(cells(7, 1), on_s)
+        quantise_z(cells(0, 2))
+        weave(cells(4, 2), on_v)
+        for cols in (cells(2, 2), cells(4, 2), cells(6, 1), cells(7, 1)):
+            quantise_z(cols)
+        for bank, (cols, mover) in enumerate(
+            ((cells(0, 2), on_s), (cells(2, 2), on_s), (cells(4, 2), on_v), (cells(6, 1), on_s), (cells(7, 1), on_v))
         ):
-            round_z(b, side, mover)
-        rows = [turn_back(block, tag, mover) for block, (tag, mover) in enumerate((("z0a", on_s), ("z1a", on_s), ("z0b", on_v), ("z1b", on_s)))]
-        for block, (tag, mover) in enumerate((("z2a", on_s), ("z3a", on_s), ("z2b", on_s), ("z3b", on_v))):
-            second_product(block, rows[block], tag, mover)
+            second_product(cols, (5 + bank) % 8, mover)

@@ -22,6 +22,7 @@ HALF = S // 2
 LIST_COLS = S // 16
 UNIT = 128
 W1_VECTOR = 80
+EARLY_SCALE_LOADS = 6
 
 
 def tile_picked_unet_none_p_kernel(
@@ -62,13 +63,17 @@ def tile_picked_unet_none_p_kernel(
         xs_rows = x_scales.bitcast(I32)
         skip_rows = skip.rearrange("(p t) v -> p t v", t=PACK)
 
+        def load_scales(n):
+            r, g = divmod(n, K_PASSES)
+            nc.sync.dma_start(out=xs_table[4 * g + r : P : 32, :].bitcast(I32), in_=xs_rows[g, r:16:4, :])
+
         nc.sync.dma_start(offs_sb[:], offs)
         nc.sync.dma_start(out=w1_raw[0][:], in_=w1_rows[0])
-        for q in range(4):
-            nc.sync.dma_start(
-                out=xs_table[32 * q : 32 * q + 4 * K_PASSES, :].bitcast(I32), in_=xs_rows[:, 4 * q : 4 * q + 4, :]
-            )
+        for n in range(EARLY_SCALE_LOADS):
+            load_scales(n)
         nc.sync.dma_start(out=x_table[0][:].bitcast(I32), in_=x_rows[0])
+        for n in range(EARLY_SCALE_LOADS, 4 * K_PASSES):
+            load_scales(n)
         nc.sync.dma_start(out=w1_raw[1][:], in_=w1_rows[1])
         nc.sync.dma_start(cell_sb[:], cell)
         nc.sync.dma_start(out=x_table[1][:].bitcast(I32), in_=x_rows[1])
@@ -126,8 +131,8 @@ def tile_picked_unet_none_p_kernel(
 
         first, second, rest = slice(0, P), slice(P, HALF), slice(P, S)
         quantise_w1(0)
-        nc.vector.tensor_copy(xs_picked[:], xs_table[:].indirect(offs_sb[:]))
         gather_words(0, whole)
+        nc.vector.tensor_copy(xs_picked[:], xs_table[:].indirect(offs_sb[:]))
         quantise_w1(1)
         for part in (first, second, halves[1]):
             gather_words(1, part)

@@ -1,6 +1,7 @@
 from contextlib import ExitStack
 
 import concourse.mybir as mybir
+from concourse.masks import make_identity
 
 K, T, S, H, N, U = 1024, 2048, 512, 512, 128, 1024
 FLOPS = 2 * K * H * S + 2 * H * N * U
@@ -21,6 +22,7 @@ K_PASSES = K // (P * PACK)
 HALF = S // 2
 LIST_COLS = S // 16
 UNIT = 128
+TURNED = 512
 W1_VECTOR = 80
 EARLY_SCALE_LOADS = 6
 
@@ -44,11 +46,11 @@ def tile_picked_unet_none_p_kernel(
         w1_raw = [keep.tile([P, PACK, H], F32, name=f"w1_raw{g}", align_bytes=64) for g in range(K_PASSES)]
         w1_codes = [keep.tile([P, H], U32, name=f"w1_codes{g}", align_bytes=64) for g in range(K_PASSES)]
         w1_plane = [keep.tile([P, H], U8, name=f"w1_plane{g}", align_bytes=64) for g in range(K_PASSES)]
-        skip_first = keep.tile([P, U], F32, align_bytes=64)
-        skip_rest = keep.tile([P, PACK - 1, U], F32, align_bytes=64)
-        skip_sb = [skip_first[:]] + [skip_rest[:, t, :] for t in range(PACK - 1)]
+        skip_pair = [keep.tile([P, 2, U], F32, name=f"skip_pair{u}", align_bytes=64) for u in range(2)]
+        skip_sb = [skip_pair[t // 2][:, t % 2, :] for t in range(PACK)]
         up = [keep.tile([P, U], F32, name=f"up{t}", align_bytes=64) for t in range(PACK)]
-        z_planes = keep.tile([P, U // UNIT, PACK, UNIT], BF16, align_bytes=64)
+        z_planes = keep.tile([P, (U - TURNED) // UNIT, PACK, UNIT], BF16, align_bytes=64)
+        ident = keep.tile([P, P], F32, align_bytes=64)
         w2_codes = keep.tile([P, N], U32, align_bytes=64)
         w2_plane = keep.tile([P, N], U8, align_bytes=64)
 
@@ -57,6 +59,7 @@ def tile_picked_unet_none_p_kernel(
         nc.vector.memset(w2_plane[:].bitcast(I32), 0)
         for t in range(1, PACK):
             nc.gpsimd.memset(up[t][:], 0.0)
+        make_identity(nc, ident[:])
 
         w1_rows = w1.rearrange("(g p j) c -> g p j c", g=K_PASSES, j=PACK)
         x_rows = x_words.rearrange("g p n t -> g p (n t)").bitcast(I32)
@@ -75,10 +78,10 @@ def tile_picked_unet_none_p_kernel(
         for n in range(EARLY_SCALE_LOADS, 4 * K_PASSES):
             load_scales(n)
         nc.sync.dma_start(out=w1_raw[1][:], in_=w1_rows[1])
-        nc.sync.dma_start(cell_sb[:], cell)
         nc.sync.dma_start(out=x_table[1][:].bitcast(I32), in_=x_rows[1])
-        nc.sync.dma_start(out=skip_first[:], in_=skip_rows[:, 0, :])
-        nc.sync.dma_start(out=skip_rest[:], in_=skip_rows[:, 1:, :])
+        nc.sync.dma_start(cell_sb[:], cell)
+        for u in range(2):
+            nc.sync.dma_start(out=skip_pair[u][:], in_=skip_rows[:, 2 * u : 2 * u + 2, :])
         nc.sync.dma_start(out=w2_codes[:].bitcast(I32), in_=w2_words[0].rearrange("p n t -> p (n t)").bitcast(I32))
         for q in range(4):
             nc.sync.dma_start(
@@ -123,7 +126,7 @@ def tile_picked_unet_none_p_kernel(
 
         def add_skip(engine, t, cols):
             engine.tensor_tensor(
-                z_planes[:, cols.start // UNIT : cols.stop // UNIT, t, :],
+                z_planes[:, (cols.start - TURNED) // UNIT : (cols.stop - TURNED) // UNIT, t, :],
                 up[t][:, cols].rearrange("p (n v) -> p n v", v=UNIT),
                 skip_sb[t][:, cols].rearrange("p (n v) -> p n v", v=UNIT),
                 ADD,
@@ -131,19 +134,17 @@ def tile_picked_unet_none_p_kernel(
 
         first, second, rest = slice(0, P), slice(P, HALF), slice(P, S)
         quantise_w1(0)
-        gather_words(0, whole)
-        nc.vector.tensor_copy(xs_picked[:], xs_table[:].indirect(offs_sb[:]))
+        for part in halves:
+            gather_words(0, part)
+            nc.vector.tensor_copy(xs_picked[:, part], xs_table[:].indirect(list_part(offs_sb, part)))
         quantise_w1(1)
         for part in (first, second, halves[1]):
             gather_words(1, part)
 
-        held = [(0, first), (0, rest), (1, whole), (2, whole), (3, whole)]
+        held = [(0, first), (0, rest), (1, halves[0]), (1, halves[1]), (2, whole), (3, whole)]
         accs = [psum.tile([P, part.stop - part.start], F32, name="h_acc", tag=f"bank{n}") for n, (t, part) in enumerate(held)]
-        steps = [
-            (0, first), (1, second), (2, halves[0]), (3, halves[0]),
-            (1, halves[1]), (2, halves[1]), (3, halves[1]), (4, whole),
-        ]
-        for g in range(K_PASSES):
+
+        def products(g, steps):
             for n, part in steps:
                 t, span = held[n]
                 first_product(
@@ -155,18 +156,24 @@ def tile_picked_unet_none_p_kernel(
                     g == K_PASSES - 1 and part.stop == span.stop,
                 )
 
+        low_steps = [(0, first), (2, halves[0]), (1, second), (4, halves[0])]
+        high_steps = [(3, halves[1]), (1, halves[1]), (4, halves[1])]
+        products(0, low_steps + [(5, halves[0])] + high_steps + [(5, halves[1])])
+        products(1, low_steps + high_steps + [(5, whole)])
+
         h = [keep.tile([P, S], F32, name=f"h{t}", align_bytes=64) for t in range(PACK)]
         on_s(out=h[0][:, first], in_=accs[0][:])
         scatter_scalar(0, first, h[0])
-        on_v(out=h[0][:, rest], in_=accs[1][:])
-        on_s(out=h[1][:], in_=accs[2][:])
-        on_v(out=h[2][:], in_=accs[3][:])
-        on_s(out=h[3][:], in_=accs[4][:])
-        scatter_vector(0, rest, h[0])
-        scatter_vector(2, whole, h[2])
+        on_v(out=h[1][:, halves[0]], in_=accs[2][:])
+        on_v(out=h[1][:, halves[1]], in_=accs[3][:])
+        on_s(out=h[0][:, rest], in_=accs[1][:])
+        on_v(out=h[2][:], in_=accs[4][:])
+        on_s(out=h[3][:], in_=accs[5][:])
+        scatter_scalar(0, rest, h[0])
+        for t in (1, 2):
+            scatter_vector(t, whole, h[t])
         for part in halves:
-            for t in (1, 3):
-                scatter_scalar(t, part, h[t])
+            scatter_scalar(3, part, h[3])
 
         def cells(first_unit, units):
             return slice(first_unit * UNIT, (first_unit + units) * UNIT)
@@ -178,7 +185,7 @@ def tile_picked_unet_none_p_kernel(
         def weave(cols, mover):
             mover(
                 out=z_bf[:, cols.start * PACK : cols.stop * PACK].rearrange("p (n c i t) -> p n c t i", c=UNIT // 4, i=4, t=PACK),
-                in_=z_planes[:, cols.start // UNIT : cols.stop // UNIT].rearrange("p n t (c i) -> p n c t i", i=4),
+                in_=z_planes[:, (cols.start - TURNED) // UNIT : (cols.stop - TURNED) // UNIT].rearrange("p n t (c i) -> p n c t i", i=4),
             )
 
         def quantise_z(cols):
@@ -202,24 +209,71 @@ def tile_picked_unet_none_p_kernel(
             mover(out=result[:], in_=acc[:])
             nc.sync.dma_start(out=out[:, cols], in_=result[:])
 
-        low, high = cells(0, 4), cells(4, 4)
-        add_skip(nc.gpsimd, 0, cells(0, 8))
-        for t in (2, 1):
-            add_skip(nc.vector, t, low)
-        add_skip(nc.vector, 3, cells(0, 1))
-        weave(cells(0, 1), on_s)
-        add_skip(nc.vector, 3, cells(1, 3))
-        weave(cells(1, 1), on_s)
-        weave(cells(2, 2), on_s)
-        for t in (2, 1, 3):
-            add_skip(nc.vector, t, high)
-        weave(cells(6, 1), on_s)
-        weave(cells(7, 1), on_s)
-        quantise_z(cells(0, 2))
-        weave(cells(4, 2), on_v)
-        for cols in (cells(2, 2), cells(4, 2), cells(6, 1), cells(7, 1)):
+        sum_banks = [
+            [psum.tile([P, 2, 2, P], F32, name="sum_bank", tag=f"bank{bank}") for bank in banks] for banks in ((6, 7), (0, 2))
+        ]
+        z_turned = [keep.tile([P, 2 * H], BF16, name=f"z_turned{side}", align_bytes=64) for side in range(2)]
+
+        def turn(source, t, side, start, stop):
+            for n in range(2):
+                nc.tensor.matmul(
+                    out=sum_banks[t // 2][side][:, n, t % 2, :],
+                    lhsT=source[:, cells(2 * side + n, 1)],
+                    rhs=ident[:],
+                    is_transpose=True,
+                    start=(start and n == 0),
+                    stop=(stop and n == 1),
+                )
+
+        def turn_pair(u):
+            for side in range(2):
+                for t in (2 * u, 2 * u + 1):
+                    turn(skip_sb[t], t, side, t % 2 == 0, False)
+            for side in range(2):
+                for t in (2 * u, 2 * u + 1):
+                    turn(up[t], t, side, False, t % 2 == 1)
+
+        def round_pair(u, side, mover):
+            mover(
+                out=z_turned[side][:].rearrange("q (n u p e) -> q u n p e", n=2, u=2, e=2)[:, u],
+                in_=sum_banks[u][side][:].rearrange("q n e p -> q n p e"),
+            )
+
+        def turn_back(side, bank):
+            back = psum.tile([P, 2, 2, P], F32, name="back_bank", tag=f"bank{bank}")
+            words = z_turned[side][:].bitcast(F32)
+            for n in range(2):
+                for u in range(2):
+                    nc.tensor.transpose(back[:, n, u, :], words[:, cells(2 * n + u, 1)], ident[:])
+            return back
+
+        def weave_words(back, side, n0, n1, mover):
+            cols = cells(2 * side + n0, n1 - n0)
+            mover(
+                out=z_bf[:, cols.start * PACK : cols.stop * PACK].bitcast(F32).rearrange("p (n q u) -> p n q u", q=P, u=2),
+                in_=back[:, n0:n1].rearrange("p n u q -> p n q u"),
+            )
+
+        high = cells(4, 4)
+        for t in (0, 1):
+            add_skip(nc.gpsimd, t, high)
+        for u in range(2):
+            turn_pair(u)
+        round_pair(0, 0, on_s)
+        round_pair(0, 1, on_s)
+        for cols in (cells(4, 2), cells(6, 2)):
+            for t in (2, 3):
+                add_skip(nc.vector, t, cols)
+        for side in range(2):
+            round_pair(1, side, on_s)
+        backs = [turn_back(side, bank) for side, bank in enumerate((1, 3))]
+        for cols in (cells(4, 2), cells(6, 2)):
+            weave(cols, on_v)
+        weave_words(backs[0], 0, 0, 2, on_s)
+        for n in range(2):
+            weave_words(backs[1], 1, n, n + 1, on_s)
+        order = (cells(4, 2), on_s), (cells(6, 2), on_s), (cells(0, 2), on_v), (cells(2, 1), on_s), (cells(3, 1), on_v)
+        for cols, mover in order:
             quantise_z(cols)
-        for bank, (cols, mover) in enumerate(
-            ((cells(0, 2), on_s), (cells(2, 2), on_s), (cells(4, 2), on_v), (cells(6, 1), on_s), (cells(7, 1), on_v))
-        ):
-            second_product(cols, (5 + bank) % 8, mover)
+        for bank, (cols, mover) in zip((2, 1, 4, 5, 6), order):
+            second_product(cols, bank, mover)

@@ -23,7 +23,7 @@ HALF = S // 2
 LIST_COLS = S // 16
 UNIT = 128
 TURNED = 512
-W1_VECTOR = 80
+W1_VECTOR = 64
 EARLY_SCALE_LOADS = 6
 
 
@@ -55,10 +55,9 @@ def tile_picked_unet_none_p_kernel(
         w2_plane = keep.tile([P, N], U8, align_bytes=64)
 
         nc.vector.memset(xs_table[:].bitcast(I32), 0)
-        nc.vector.memset(up[0][:], 0.0)
+        for t in range(PACK):
+            nc.vector.memset(up[t][:].bitcast(I32), 0)
         nc.vector.memset(w2_plane[:].bitcast(I32), 0)
-        for t in range(1, PACK):
-            nc.gpsimd.memset(up[t][:], 0.0)
         make_identity(nc, ident[:])
 
         w1_rows = w1.rearrange("(g p j) c -> g p j c", g=K_PASSES, j=PACK)
@@ -77,9 +76,9 @@ def tile_picked_unet_none_p_kernel(
         nc.sync.dma_start(out=x_table[0][:].bitcast(I32), in_=x_rows[0])
         for n in range(EARLY_SCALE_LOADS, 4 * K_PASSES):
             load_scales(n)
+        nc.sync.dma_start(cell_sb[:], cell)
         nc.sync.dma_start(out=w1_raw[1][:], in_=w1_rows[1])
         nc.sync.dma_start(out=x_table[1][:].bitcast(I32), in_=x_rows[1])
-        nc.sync.dma_start(cell_sb[:], cell)
         for u in range(2):
             nc.sync.dma_start(out=skip_pair[u][:], in_=skip_rows[:, 2 * u : 2 * u + 2, :])
         nc.sync.dma_start(out=w2_codes[:].bitcast(I32), in_=w2_words[0].rearrange("p n t -> p (n t)").bitcast(I32))
@@ -134,9 +133,8 @@ def tile_picked_unet_none_p_kernel(
 
         first, second, rest = slice(0, P), slice(P, HALF), slice(P, S)
         quantise_w1(0)
-        for part in halves:
-            gather_words(0, part)
-            nc.vector.tensor_copy(xs_picked[:, part], xs_table[:].indirect(list_part(offs_sb, part)))
+        gather_words(0, whole)
+        nc.vector.tensor_copy(xs_picked[:], xs_table[:].indirect(offs_sb[:]))
         quantise_w1(1)
         for part in (first, second, halves[1]):
             gather_words(1, part)
@@ -158,8 +156,8 @@ def tile_picked_unet_none_p_kernel(
 
         low_steps = [(0, first), (2, halves[0]), (1, second), (4, halves[0])]
         high_steps = [(3, halves[1]), (1, halves[1]), (4, halves[1])]
-        products(0, low_steps + [(5, halves[0])] + high_steps + [(5, halves[1])])
-        products(1, low_steps + high_steps + [(5, whole)])
+        for g in range(K_PASSES):
+            products(g, low_steps + high_steps + [(5, whole)])
 
         h = [keep.tile([P, S], F32, name=f"h{t}", align_bytes=64) for t in range(PACK)]
         on_s(out=h[0][:, first], in_=accs[0][:])

@@ -46,8 +46,8 @@ def tile_picked_unet_none_p_kernel(
         w1_raw = [keep.tile([P, PACK, H], F32, name=f"w1_raw{g}", align_bytes=64) for g in range(K_PASSES)]
         w1_codes = [keep.tile([P, H], U32, name=f"w1_codes{g}", align_bytes=64) for g in range(K_PASSES)]
         w1_plane = [keep.tile([P, H], U8, name=f"w1_plane{g}", align_bytes=64) for g in range(K_PASSES)]
-        skip_pair = [keep.tile([P, 2, U], F32, name=f"skip_pair{u}", align_bytes=64) for u in range(2)]
-        skip_sb = [skip_pair[t // 2][:, t % 2, :] for t in range(PACK)]
+        skip_all = keep.tile([P, PACK, U], F32, align_bytes=64)
+        skip_sb = [skip_all[:, t, :] for t in range(PACK)]
         up = [keep.tile([P, U], F32, name=f"up{t}", align_bytes=64) for t in range(PACK)]
         z_planes = keep.tile([P, (U - TURNED) // UNIT, PACK, UNIT], BF16, align_bytes=64)
         ident = keep.tile([P, P], F32, align_bytes=64)
@@ -79,8 +79,7 @@ def tile_picked_unet_none_p_kernel(
         nc.sync.dma_start(cell_sb[:], cell)
         nc.sync.dma_start(out=w1_raw[1][:], in_=w1_rows[1])
         nc.sync.dma_start(out=x_table[1][:].bitcast(I32), in_=x_rows[1])
-        for u in range(2):
-            nc.sync.dma_start(out=skip_pair[u][:], in_=skip_rows[:, 2 * u : 2 * u + 2, :])
+        nc.sync.dma_start(out=skip_all[:], in_=skip_rows)
         nc.sync.dma_start(out=w2_codes[:].bitcast(I32), in_=w2_words[0].rearrange("p n t -> p (n t)").bitcast(I32))
         for q in range(4):
             nc.sync.dma_start(
@@ -139,10 +138,16 @@ def tile_picked_unet_none_p_kernel(
         for part in (first, second, halves[1]):
             gather_words(1, part)
 
-        held = [(0, first), (0, rest), (1, halves[0]), (1, halves[1]), (2, whole), (3, whole)]
-        accs = [psum.tile([P, part.stop - part.start], F32, name="h_acc", tag=f"bank{n}") for n, (t, part) in enumerate(held)]
-
-        def products(g, steps):
+        starters = psum.tile([P, 2, P], F32, name="h_acc", tag="bank0")
+        held = [(0, rest), (1, halves[0]), (1, halves[1]), (2, halves[0]), (2, halves[1]), (3, rest)]
+        accs = [psum.tile([P, part.stop - part.start], F32, name="h_acc", tag=f"bank{n + 1}") for n, (t, part) in enumerate(held)]
+        steps = [
+            (1, halves[0]), (3, halves[0]), (0, second), (5, second),
+            (2, halves[1]), (4, halves[1]), (0, halves[1]), (5, halves[1]),
+        ]
+        for g in range(K_PASSES):
+            for n, t in enumerate((0, 3)):
+                first_product(t, first, starters[:, n, :], g, g == 0 and n == 0, g == K_PASSES - 1 and n == 1)
             for n, part in steps:
                 t, span = held[n]
                 first_product(
@@ -154,24 +159,20 @@ def tile_picked_unet_none_p_kernel(
                     g == K_PASSES - 1 and part.stop == span.stop,
                 )
 
-        low_steps = [(0, first), (2, halves[0]), (1, second), (4, halves[0])]
-        high_steps = [(3, halves[1]), (1, halves[1]), (4, halves[1])]
-        for g in range(K_PASSES):
-            products(g, low_steps + high_steps + [(5, whole)])
-
         h = [keep.tile([P, S], F32, name=f"h{t}", align_bytes=64) for t in range(PACK)]
-        on_s(out=h[0][:, first], in_=accs[0][:])
-        scatter_scalar(0, first, h[0])
-        on_v(out=h[1][:, halves[0]], in_=accs[2][:])
-        on_v(out=h[1][:, halves[1]], in_=accs[3][:])
-        on_s(out=h[0][:, rest], in_=accs[1][:])
-        on_v(out=h[2][:], in_=accs[4][:])
-        on_s(out=h[3][:], in_=accs[5][:])
-        scatter_scalar(0, rest, h[0])
-        for t in (1, 2):
-            scatter_vector(t, whole, h[t])
-        for part in halves:
-            scatter_scalar(3, part, h[3])
+        for n, t in enumerate((0, 3)):
+            on_s(out=h[t][:, first], in_=starters[:, n, :])
+        for t in (0, 3):
+            scatter_scalar(t, first, h[t])
+        for t, n in ((0, 0), (3, 5)):
+            on_s(out=h[t][:, rest], in_=accs[n][:])
+        for t in (0, 3):
+            scatter_scalar(t, rest, h[t])
+        for side, part in enumerate(halves):
+            for t in (1, 2):
+                on_v(out=h[t][:, part], in_=accs[2 * t - 1 + side][:])
+            scatter_vector(1, part, h[1])
+        scatter_vector(2, whole, h[2])
 
         def cells(first_unit, units):
             return slice(first_unit * UNIT, (first_unit + units) * UNIT)
@@ -208,7 +209,7 @@ def tile_picked_unet_none_p_kernel(
             nc.sync.dma_start(out=out[:, cols], in_=result[:])
 
         sum_banks = [
-            [psum.tile([P, 2, 2, P], F32, name="sum_bank", tag=f"bank{bank}") for bank in banks] for banks in ((6, 7), (0, 2))
+            [psum.tile([P, 2, 2, P], F32, name="sum_bank", tag=f"bank{bank}") for bank in banks] for banks in ((7, 0), (2, 4))
         ]
         z_turned = [keep.tile([P, 2 * H], BF16, name=f"z_turned{side}", align_bytes=64) for side in range(2)]
 
@@ -223,10 +224,12 @@ def tile_picked_unet_none_p_kernel(
                     stop=(stop and n == 1),
                 )
 
-        def turn_pair(u):
+        def turn_skip(u):
             for side in range(2):
                 for t in (2 * u, 2 * u + 1):
                     turn(skip_sb[t], t, side, t % 2 == 0, False)
+
+        def turn_pair(u):
             for side in range(2):
                 for t in (2 * u, 2 * u + 1):
                     turn(up[t], t, side, False, t % 2 == 1)
@@ -237,13 +240,10 @@ def tile_picked_unet_none_p_kernel(
                 in_=sum_banks[u][side][:].rearrange("q n e p -> q n p e"),
             )
 
-        def turn_back(side, bank):
-            back = psum.tile([P, 2, 2, P], F32, name="back_bank", tag=f"bank{bank}")
+        def turn_back(back, side, u):
             words = z_turned[side][:].bitcast(F32)
             for n in range(2):
-                for u in range(2):
-                    nc.tensor.transpose(back[:, n, u, :], words[:, cells(2 * n + u, 1)], ident[:])
-            return back
+                nc.tensor.transpose(back[:, n, u, :], words[:, cells(2 * n + u, 1)], ident[:])
 
         def weave_words(back, side, n0, n1, mover):
             cols = cells(2 * side + n0, n1 - n0)
@@ -253,18 +253,23 @@ def tile_picked_unet_none_p_kernel(
             )
 
         high = cells(4, 4)
-        for t in (0, 1):
+        for t in (1, 0):
             add_skip(nc.gpsimd, t, high)
+        for u in range(2):
+            turn_skip(u)
         for u in range(2):
             turn_pair(u)
         round_pair(0, 0, on_s)
         round_pair(0, 1, on_s)
         for cols in (cells(4, 2), cells(6, 2)):
-            for t in (2, 3):
+            for t in (3, 2):
                 add_skip(nc.vector, t, cols)
         for side in range(2):
             round_pair(1, side, on_s)
-        backs = [turn_back(side, bank) for side, bank in enumerate((1, 3))]
+        backs = [psum.tile([P, 2, 2, P], F32, name="back_bank", tag=f"bank{bank}") for bank in (1, 3)]
+        for u in range(2):
+            for side in range(2):
+                turn_back(backs[side], side, u)
         for cols in (cells(4, 2), cells(6, 2)):
             weave(cols, on_v)
         weave_words(backs[0], 0, 0, 2, on_s)
@@ -273,5 +278,5 @@ def tile_picked_unet_none_p_kernel(
         order = (cells(4, 2), on_s), (cells(6, 2), on_s), (cells(0, 2), on_v), (cells(2, 1), on_s), (cells(3, 1), on_v)
         for cols, mover in order:
             quantise_z(cols)
-        for bank, (cols, mover) in zip((2, 1, 4, 5, 6), order):
+        for bank, (cols, mover) in zip((4, 1, 5, 6, 7), order):
             second_product(cols, bank, mover)

@@ -23,8 +23,8 @@ HALF = S // 2
 LIST_COLS = S // 16
 UNIT = 128
 TURNED = 512
-W1_VECTOR = 64
-EARLY_SCALE_LOADS = 6
+W1_VECTOR = 80
+EARLY_SCALE_LOADS = 5
 
 
 def tile_picked_unet_none_p_kernel(
@@ -69,8 +69,8 @@ def tile_picked_unet_none_p_kernel(
             r, g = divmod(n, K_PASSES)
             nc.sync.dma_start(out=xs_table[4 * g + r : P : 32, :].bitcast(I32), in_=xs_rows[g, r:16:4, :])
 
-        nc.sync.dma_start(offs_sb[:], offs)
         nc.sync.dma_start(out=w1_raw[0][:], in_=w1_rows[0])
+        nc.sync.dma_start(offs_sb[:], offs)
         for n in range(EARLY_SCALE_LOADS):
             load_scales(n)
         nc.sync.dma_start(out=x_table[0][:].bitcast(I32), in_=x_rows[0])
@@ -138,7 +138,7 @@ def tile_picked_unet_none_p_kernel(
         for part in (first, second, halves[1]):
             gather_words(1, part)
 
-        starters = psum.tile([P, 2, P], F32, name="h_acc", tag="bank0")
+        starters = [psum.tile([P, P], F32, name="h_acc", tag=f"bank{bank}") for bank in (0, 7)]
         held = [(0, rest), (1, halves[0]), (1, halves[1]), (2, halves[0]), (2, halves[1]), (3, rest)]
         accs = [psum.tile([P, part.stop - part.start], F32, name="h_acc", tag=f"bank{n + 1}") for n, (t, part) in enumerate(held)]
         steps = [
@@ -147,7 +147,7 @@ def tile_picked_unet_none_p_kernel(
         ]
         for g in range(K_PASSES):
             for n, t in enumerate((0, 3)):
-                first_product(t, first, starters[:, n, :], g, g == 0 and n == 0, g == K_PASSES - 1 and n == 1)
+                first_product(t, first, starters[n][:], g, g == 0, g == K_PASSES - 1)
             for n, part in steps:
                 t, span = held[n]
                 first_product(
@@ -161,7 +161,7 @@ def tile_picked_unet_none_p_kernel(
 
         h = [keep.tile([P, S], F32, name=f"h{t}", align_bytes=64) for t in range(PACK)]
         for n, t in enumerate((0, 3)):
-            on_s(out=h[t][:, first], in_=starters[:, n, :])
+            on_s(out=h[t][:, first], in_=starters[n][:])
         for t in (0, 3):
             scatter_scalar(t, first, h[t])
         for t, n in ((0, 0), (3, 5)):

@@ -22,6 +22,7 @@ K_PASSES = K // (P * PACK)
 HALF = S // 2
 LIST_COLS = S // 16
 UNIT = 128
+BLOCK = 256
 TURNED = 512
 W1_VECTOR = 80
 EARLY_SCALE_LOADS = 5
@@ -49,7 +50,7 @@ def tile_picked_unet_none_p_kernel(
         skip_all = keep.tile([P, PACK, U], F32, align_bytes=64)
         skip_sb = [skip_all[:, t, :] for t in range(PACK)]
         up = [keep.tile([P, U], F32, name=f"up{t}", align_bytes=64) for t in range(PACK)]
-        z_planes = keep.tile([P, (U - TURNED) // UNIT, PACK, UNIT], BF16, align_bytes=64)
+        z_planes = keep.tile([P, (U - TURNED) // BLOCK, PACK, BLOCK], BF16, align_bytes=64)
         ident = keep.tile([P, P], F32, align_bytes=64)
         w2_codes = keep.tile([P, N], U32, align_bytes=64)
         w2_plane = keep.tile([P, N], U8, align_bytes=64)
@@ -124,9 +125,9 @@ def tile_picked_unet_none_p_kernel(
 
         def add_skip(engine, t, cols):
             engine.tensor_tensor(
-                z_planes[:, (cols.start - TURNED) // UNIT : (cols.stop - TURNED) // UNIT, t, :],
-                up[t][:, cols].rearrange("p (n v) -> p n v", v=UNIT),
-                skip_sb[t][:, cols].rearrange("p (n v) -> p n v", v=UNIT),
+                z_planes[:, (cols.start - TURNED) // BLOCK : (cols.stop - TURNED) // BLOCK, t, :],
+                up[t][:, cols].rearrange("p (n v) -> p n v", v=BLOCK),
+                skip_sb[t][:, cols].rearrange("p (n v) -> p n v", v=BLOCK),
                 ADD,
             )
 
@@ -183,8 +184,8 @@ def tile_picked_unet_none_p_kernel(
 
         def weave(cols, mover):
             mover(
-                out=z_bf[:, cols.start * PACK : cols.stop * PACK].rearrange("p (n c i t) -> p n c t i", c=UNIT // 4, i=4, t=PACK),
-                in_=z_planes[:, (cols.start - TURNED) // UNIT : (cols.stop - TURNED) // UNIT].rearrange("p n t (c i) -> p n c t i", i=4),
+                out=z_bf[:, cols.start * PACK : cols.stop * PACK].rearrange("p (c i t) -> p c t i", i=4, t=PACK),
+                in_=z_planes[:, (cols.start - TURNED) // BLOCK].rearrange("p t (c i) -> p c t i", i=4),
             )
 
         def quantise_z(cols):

@@ -21,9 +21,11 @@ PACK = 4
 K_PASSES = K // (P * PACK)
 HALF = S // 2
 LIST_COLS = S // 16
+SCALE_ROWS = 16
 UNIT = 128
-BLOCK = 256
-TURNED = 512
+BLOCK = 2 * UNIT
+TURNED = 2 * BLOCK
+LINE = 4
 W1_VECTOR = 80
 EARLY_SCALE_LOADS = 5
 
@@ -46,19 +48,19 @@ def tile_picked_unet_none_p_kernel(
         xs_picked = keep.tile([P, S], U8, align_bytes=64)
         w1_raw = [keep.tile([P, PACK, H], F32, name=f"w1_raw{g}", align_bytes=64) for g in range(K_PASSES)]
         w1_codes = [keep.tile([P, H], U32, name=f"w1_codes{g}", align_bytes=64) for g in range(K_PASSES)]
-        w1_plane = [keep.tile([P, H], U8, name=f"w1_plane{g}", align_bytes=64) for g in range(K_PASSES)]
+        w1_scales = [keep.tile([P, H], U8, name=f"w1_scales{g}", align_bytes=64) for g in range(K_PASSES)]
         skip_all = keep.tile([P, PACK, U], F32, align_bytes=64)
         skip_sb = [skip_all[:, t, :] for t in range(PACK)]
         up = [keep.tile([P, U], F32, name=f"up{t}", align_bytes=64) for t in range(PACK)]
         z_planes = keep.tile([P, (U - TURNED) // BLOCK, PACK, BLOCK], BF16, align_bytes=64)
         ident = keep.tile([P, P], F32, align_bytes=64)
         w2_codes = keep.tile([P, N], U32, align_bytes=64)
-        w2_plane = keep.tile([P, N], U8, align_bytes=64)
+        w2_scale_sb = keep.tile([P, N], U8, align_bytes=64)
 
         nc.vector.memset(xs_table[:].bitcast(I32), 0)
         for t in range(PACK):
             nc.vector.memset(up[t][:].bitcast(I32), 0)
-        nc.vector.memset(w2_plane[:].bitcast(I32), 0)
+        nc.vector.memset(w2_scale_sb[:].bitcast(I32), 0)
         make_identity(nc, ident[:])
 
         w1_rows = w1.rearrange("(g p j) c -> g p j c", g=K_PASSES, j=PACK)
@@ -68,7 +70,7 @@ def tile_picked_unet_none_p_kernel(
 
         def load_scales(n):
             r, g = divmod(n, K_PASSES)
-            nc.sync.dma_start(out=xs_table[4 * g + r : P : 32, :].bitcast(I32), in_=xs_rows[g, r:16:4, :])
+            nc.sync.dma_start(out=xs_table[4 * g + r : P : 32, :].bitcast(I32), in_=xs_rows[g, r:SCALE_ROWS:4, :])
 
         nc.sync.dma_start(out=w1_raw[0][:], in_=w1_rows[0])
         nc.sync.dma_start(offs_sb[:], offs)
@@ -84,12 +86,15 @@ def tile_picked_unet_none_p_kernel(
         nc.sync.dma_start(out=w2_codes[:].bitcast(I32), in_=w2_words[0].rearrange("p n t -> p (n t)").bitcast(I32))
         for q in range(4):
             nc.sync.dma_start(
-                out=w2_plane[32 * q : 32 * q + 4, :].bitcast(I32), in_=w2_scales[0, 4 * q : 4 * q + 4, :].bitcast(I32)
+                out=w2_scale_sb[32 * q : 32 * q + 4, :].bitcast(I32),
+                in_=w2_scales[0, 4 * q : 4 * q + 4, :].bitcast(I32),
             )
 
-        on_s, on_v = nc.scalar.copy, nc.vector.tensor_copy
-        halves = slice(0, HALF), slice(HALF, S)
+        on_scalar, on_vector = nc.scalar.copy, nc.vector.tensor_copy
+
         whole = slice(0, S)
+        halves = slice(0, HALF), slice(HALF, S)
+        first, second, rest = slice(0, P), slice(P, HALF), slice(P, S)
 
         def list_part(tile, part):
             return tile[:, part.start // 16 : part.stop // 16]
@@ -98,9 +103,9 @@ def tile_picked_unet_none_p_kernel(
             grouped = keep.tile([P, H * PACK], BF16, name=f"w1_bf{g}", align_bytes=64)
             dealt = grouped[:].rearrange("p (t m j) -> p m j t", t=PACK, j=PACK)
             raw = w1_raw[g][:].rearrange("p j (m t) -> p m j t", t=PACK)
-            on_v(out=dealt[:, :W1_VECTOR], in_=raw[:, :W1_VECTOR])
-            on_s(out=dealt[:, W1_VECTOR:], in_=raw[:, W1_VECTOR:])
-            nc.vector.quantize_mx(out=w1_codes[g][:].bitcast(FP8X4), scales=w1_plane[g][:], in_=grouped[:])
+            on_vector(out=dealt[:, :W1_VECTOR], in_=raw[:, :W1_VECTOR])
+            on_scalar(out=dealt[:, W1_VECTOR:], in_=raw[:, W1_VECTOR:])
+            nc.vector.quantize_mx(out=w1_codes[g][:].bitcast(FP8X4), scales=w1_scales[g][:], in_=grouped[:])
 
         def gather_words(g, part):
             nc.vector.tensor_copy(x_picked[g][:, part], x_table[g][:].indirect(list_part(offs_sb, part)))
@@ -110,45 +115,35 @@ def tile_picked_unet_none_p_kernel(
             nc.tensor.matmul_mx(
                 out=acc,
                 lhsT=w1_codes[g][:, cols].bitcast(FP8X4),
-                lhsT_scale=w1_plane[g][:, cols],
+                lhsT_scale=w1_scales[g][:, cols],
                 rhs=x_picked[g][:, part].bitcast(FP8X4),
                 rhs_scale=xs_picked[4 * g : P, part],
                 start=start,
                 stop=stop,
             )
 
-        def scatter_vector(t, part, h):
-            nc.vector.tensor_copy(up[t][:].indirect(list_part(cell_sb, part)), h[:, part])
-
-        def scatter_scalar(t, part, h):
-            nc.scalar.activation(up[t][:].indirect(list_part(cell_sb, part)), h[:, part], COPY)
-
-        def add_skip(engine, t, cols):
-            engine.tensor_tensor(
-                z_planes[:, (cols.start - TURNED) // BLOCK : (cols.stop - TURNED) // BLOCK, t, :],
-                up[t][:, cols].rearrange("p (n v) -> p n v", v=BLOCK),
-                skip_sb[t][:, cols].rearrange("p (n v) -> p n v", v=BLOCK),
-                ADD,
-            )
-
-        first, second, rest = slice(0, P), slice(P, HALF), slice(P, S)
         quantise_w1(0)
         gather_words(0, whole)
-        nc.vector.tensor_copy(xs_picked[:], xs_table[:].indirect(offs_sb[:]))
+        for part in halves:
+            nc.vector.tensor_copy(xs_picked[:, part], xs_table[:].indirect(list_part(offs_sb, part)))
         quantise_w1(1)
         for part in (first, second, halves[1]):
             gather_words(1, part)
 
+        scalar_planes, vector_planes = (0, 3), (1, 2)
         starters = [psum.tile([P, P], F32, name="h_acc", tag=f"bank{bank}") for bank in (0, 7)]
         held = [(0, rest), (1, halves[0]), (1, halves[1]), (2, halves[0]), (2, halves[1]), (3, rest)]
-        accs = [psum.tile([P, part.stop - part.start], F32, name="h_acc", tag=f"bank{n + 1}") for n, (t, part) in enumerate(held)]
+        accs = [
+            psum.tile([P, span.stop - span.start], F32, name="h_acc", tag=f"bank{n + 1}")
+            for n, (t, span) in enumerate(held)
+        ]
         steps = [
             (1, halves[0]), (3, halves[0]), (0, second), (5, second),
             (2, halves[1]), (4, halves[1]), (0, halves[1]), (5, halves[1]),
         ]
         for g in range(K_PASSES):
-            for n, t in enumerate((0, 3)):
-                first_product(t, first, starters[n][:], g, g == 0, g == K_PASSES - 1)
+            for starter, t in zip(starters, scalar_planes):
+                first_product(t, first, starter[:], g, g == 0, g == K_PASSES - 1)
             for n, part in steps:
                 t, span = held[n]
                 first_product(
@@ -161,37 +156,87 @@ def tile_picked_unet_none_p_kernel(
                 )
 
         h = [keep.tile([P, S], F32, name=f"h{t}", align_bytes=64) for t in range(PACK)]
-        for n, t in enumerate((0, 3)):
-            on_s(out=h[t][:, first], in_=starters[n][:])
-        for t in (0, 3):
-            scatter_scalar(t, first, h[t])
-        for t, n in ((0, 0), (3, 5)):
-            on_s(out=h[t][:, rest], in_=accs[n][:])
-        for t in (0, 3):
-            scatter_scalar(t, rest, h[t])
-        for side, part in enumerate(halves):
-            for t in (1, 2):
-                on_v(out=h[t][:, part], in_=accs[2 * t - 1 + side][:])
-            scatter_vector(1, part, h[1])
-        scatter_vector(2, whole, h[2])
+
+        def scatter_vector(t, part):
+            nc.vector.tensor_copy(up[t][:].indirect(list_part(cell_sb, part)), h[t][:, part])
+
+        def scatter_scalar(t, part):
+            nc.scalar.activation(up[t][:].indirect(list_part(cell_sb, part)), h[t][:, part], COPY)
+
+        for part, sources in ((first, starters), (rest, (accs[0], accs[-1]))):
+            for t, source in zip(scalar_planes, sources):
+                on_scalar(out=h[t][:, part], in_=source[:])
+            for t in scalar_planes:
+                scatter_scalar(t, part)
+        for part in halves:
+            for t in vector_planes:
+                on_vector(out=h[t][:, part], in_=accs[held.index((t, part))][:])
+            scatter_vector(1, part)
+        scatter_vector(2, whole)
+
+        z_bf = keep.tile([P, U * PACK], BF16, align_bytes=64)
+        z_codes = keep.tile([P, U], U32, align_bytes=64)
+        z_scales = keep.tile([P, U], U8, align_bytes=64)
 
         def cells(first_unit, units):
             return slice(first_unit * UNIT, (first_unit + units) * UNIT)
 
-        z_bf = keep.tile([P, U * PACK], BF16, align_bytes=64)
-        z_codes = keep.tile([P, U], U32, align_bytes=64)
-        z_plane = keep.tile([P, U], U8, align_bytes=64)
+        def woven(cols):
+            return z_bf[:, cols.start * PACK : cols.stop * PACK]
 
-        def weave(cols, mover):
-            mover(
-                out=z_bf[:, cols.start * PACK : cols.stop * PACK].rearrange("p (c i t) -> p c t i", i=4, t=PACK),
-                in_=z_planes[:, (cols.start - TURNED) // BLOCK].rearrange("p t (c i) -> p c t i", i=4),
+        def add_skip(engine, t, cols):
+            engine.tensor_tensor(
+                z_planes[:, (cols.start - TURNED) // BLOCK : (cols.stop - TURNED) // BLOCK, t, :],
+                up[t][:, cols].rearrange("p (n v) -> p n v", v=BLOCK),
+                skip_sb[t][:, cols].rearrange("p (n v) -> p n v", v=BLOCK),
+                ADD,
+            )
+
+        def weave_planes(cols):
+            on_vector(
+                out=woven(cols).rearrange("p (c i t) -> p c t i", i=LINE, t=PACK),
+                in_=z_planes[:, (cols.start - TURNED) // BLOCK].rearrange("p t (c i) -> p c t i", i=LINE),
+            )
+
+        sum_banks = [
+            [psum.tile([P, 2, 2, P], F32, name="sum_bank", tag=f"bank{bank}") for bank in banks]
+            for banks in ((7, 0), (2, 4))
+        ]
+        z_turned = [keep.tile([P, 2 * H], BF16, name=f"z_turned{b}", align_bytes=64) for b in range(2)]
+
+        def turn(sources, adding):
+            for u in range(2):
+                for b in range(2):
+                    for e in range(2):
+                        for n in range(2):
+                            nc.tensor.matmul(
+                                out=sum_banks[u][b][:, n, e, :],
+                                lhsT=sources[2 * u + e][:, cells(2 * b + n, 1)],
+                                rhs=ident[:],
+                                is_transpose=True,
+                                start=(not adding and e == 0 and n == 0),
+                                stop=(adding and e == 1 and n == 1),
+                            )
+
+        def round_pair(u, b):
+            on_scalar(
+                out=z_turned[b][:].rearrange("q (n u p e) -> q u n p e", n=2, u=2, e=2)[:, u],
+                in_=sum_banks[u][b][:].rearrange("q n e p -> q n p e"),
+            )
+
+        def turn_back(back, b, u):
+            words = z_turned[b][:].bitcast(F32)
+            for n in range(2):
+                nc.tensor.transpose(back[:, n, u, :], words[:, (2 * n + u) * P : (2 * n + u + 1) * P], ident[:])
+
+        def weave_words(back, b, n0, n1):
+            on_scalar(
+                out=woven(cells(2 * b + n0, n1 - n0)).bitcast(F32).rearrange("p (n q u) -> p n q u", q=UNIT, u=2),
+                in_=back[:, n0:n1].rearrange("p n u q -> p n q u"),
             )
 
         def quantise_z(cols):
-            nc.vector.quantize_mx(
-                out=z_codes[:, cols].bitcast(FP8X4), scales=z_plane[:, cols], in_=z_bf[:, cols.start * PACK : cols.stop * PACK]
-            )
+            nc.vector.quantize_mx(out=z_codes[:, cols].bitcast(FP8X4), scales=z_scales[:, cols], in_=woven(cols))
 
         def second_product(cols, bank, mover):
             width = cols.stop - cols.start
@@ -199,9 +244,9 @@ def tile_picked_unet_none_p_kernel(
             nc.tensor.matmul_mx(
                 out=acc[:],
                 lhsT=w2_codes[:].bitcast(FP8X4),
-                lhsT_scale=w2_plane[:],
+                lhsT_scale=w2_scale_sb[:],
                 rhs=z_codes[:, cols].bitcast(FP8X4),
-                rhs_scale=z_plane[:, cols],
+                rhs_scale=z_scales[:, cols],
                 start=True,
                 stop=True,
             )
@@ -209,75 +254,36 @@ def tile_picked_unet_none_p_kernel(
             mover(out=result[:], in_=acc[:])
             nc.sync.dma_start(out=out[:, cols], in_=result[:])
 
-        sum_banks = [
-            [psum.tile([P, 2, 2, P], F32, name="sum_bank", tag=f"bank{bank}") for bank in banks] for banks in ((7, 0), (2, 4))
-        ]
-        z_turned = [keep.tile([P, 2 * H], BF16, name=f"z_turned{side}", align_bytes=64) for side in range(2)]
-
-        def turn(source, t, side, start, stop):
-            for n in range(2):
-                nc.tensor.matmul(
-                    out=sum_banks[t // 2][side][:, n, t % 2, :],
-                    lhsT=source[:, cells(2 * side + n, 1)],
-                    rhs=ident[:],
-                    is_transpose=True,
-                    start=(start and n == 0),
-                    stop=(stop and n == 1),
-                )
-
-        def turn_skip(u):
-            for side in range(2):
-                for t in (2 * u, 2 * u + 1):
-                    turn(skip_sb[t], t, side, t % 2 == 0, False)
-
-        def turn_pair(u):
-            for side in range(2):
-                for t in (2 * u, 2 * u + 1):
-                    turn(up[t], t, side, False, t % 2 == 1)
-
-        def round_pair(u, side, mover):
-            mover(
-                out=z_turned[side][:].rearrange("q (n u p e) -> q u n p e", n=2, u=2, e=2)[:, u],
-                in_=sum_banks[u][side][:].rearrange("q n e p -> q n p e"),
-            )
-
-        def turn_back(back, side, u):
-            words = z_turned[side][:].bitcast(F32)
-            for n in range(2):
-                nc.tensor.transpose(back[:, n, u, :], words[:, cells(2 * n + u, 1)], ident[:])
-
-        def weave_words(back, side, n0, n1, mover):
-            cols = cells(2 * side + n0, n1 - n0)
-            mover(
-                out=z_bf[:, cols.start * PACK : cols.stop * PACK].bitcast(F32).rearrange("p (n q u) -> p n q u", q=P, u=2),
-                in_=back[:, n0:n1].rearrange("p n u q -> p n q u"),
-            )
-
-        high = cells(4, 4)
+        high_blocks = cells(4, 2), cells(6, 2)
         for t in (1, 0):
-            add_skip(nc.gpsimd, t, high)
-        for u in range(2):
-            turn_skip(u)
-        for u in range(2):
-            turn_pair(u)
-        round_pair(0, 0, on_s)
-        round_pair(0, 1, on_s)
-        for cols in (cells(4, 2), cells(6, 2)):
+            add_skip(nc.gpsimd, t, slice(TURNED, U))
+        turn(skip_sb, adding=False)
+        turn(up, adding=True)
+        for b in range(2):
+            round_pair(0, b)
+        for cols in high_blocks:
             for t in (3, 2):
                 add_skip(nc.vector, t, cols)
-        for side in range(2):
-            round_pair(1, side, on_s)
+        for b in range(2):
+            round_pair(1, b)
         backs = [psum.tile([P, 2, 2, P], F32, name="back_bank", tag=f"bank{bank}") for bank in (1, 3)]
         for u in range(2):
-            for side in range(2):
-                turn_back(backs[side], side, u)
-        for cols in (cells(4, 2), cells(6, 2)):
-            weave(cols, on_v)
-        weave_words(backs[0], 0, 0, 2, on_s)
+            for b in range(2):
+                turn_back(backs[b], b, u)
+        for cols in high_blocks:
+            weave_planes(cols)
+        weave_words(backs[0], 0, 0, 2)
         for n in range(2):
-            weave_words(backs[1], 1, n, n + 1, on_s)
-        order = (cells(4, 2), on_s), (cells(6, 2), on_s), (cells(0, 2), on_v), (cells(2, 1), on_s), (cells(3, 1), on_v)
-        for cols, mover in order:
+            weave_words(backs[1], 1, n, n + 1)
+
+        order = (
+            (high_blocks[0], 4, on_scalar),
+            (high_blocks[1], 1, on_scalar),
+            (cells(0, 2), 5, on_vector),
+            (cells(2, 1), 6, on_scalar),
+            (cells(3, 1), 7, on_vector),
+        )
+        for cols, bank, mover in order:
             quantise_z(cols)
-        for bank, (cols, mover) in zip((4, 1, 5, 6, 7), order):
+        for cols, bank, mover in order:
             second_product(cols, bank, mover)

@@ -163,15 +163,23 @@ def tile_picked_unet_none_p_kernel(
         def scatter_scalar(t, part):
             nc.scalar.activation(up[t][:].indirect(list_part(cell_sb, part)), h[t][:, part], COPY)
 
-        for part, sources in ((first, starters), (rest, (accs[0], accs[-1]))):
-            for t, source in zip(scalar_planes, sources):
-                on_scalar(out=h[t][:, part], in_=source[:])
-            for t in scalar_planes:
-                scatter_scalar(t, part)
-        for part in halves:
-            for t in vector_planes:
-                on_vector(out=h[t][:, part], in_=accs[held.index((t, part))][:])
-            scatter_vector(1, part)
+        def leave_psum(mover, t, part):
+            mover(out=h[t][:, part], in_=accs[held.index((t, part))][:])
+
+        for t, starter in zip(scalar_planes, starters):
+            on_scalar(out=h[t][:, first], in_=starter[:])
+        for t in scalar_planes:
+            scatter_scalar(t, first)
+        for t in vector_planes:
+            leave_psum(on_vector, t, halves[0])
+        scatter_vector(1, halves[0])
+        leave_psum(on_scalar, 1, halves[1])
+        for t in scalar_planes:
+            leave_psum(on_scalar, t, rest)
+        for t in scalar_planes:
+            scatter_scalar(t, rest)
+        leave_psum(on_vector, 2, halves[1])
+        scatter_vector(1, halves[1])
         scatter_vector(2, whole)
 
         z_bf = keep.tile([P, U * PACK], BF16, align_bytes=64)
@@ -198,41 +206,38 @@ def tile_picked_unet_none_p_kernel(
                 in_=z_planes[:, (cols.start - TURNED) // BLOCK].rearrange("p t (c i) -> p c t i", i=LINE),
             )
 
-        sum_banks = [
-            [psum.tile([P, 2, 2, P], F32, name="sum_bank", tag=f"bank{bank}") for bank in banks]
-            for banks in ((7, 0), (2, 4))
-        ]
-        z_turned = [keep.tile([P, 2 * H], BF16, name=f"z_turned{b}", align_bytes=64) for b in range(2)]
+        early_sums = [psum.tile([P, 2, 2, P], F32, name="early_sum", tag=f"bank{bank}") for bank in (7, 0)]
+        late_sums = [psum.tile([P, 1, 2, P], F32, name="late_sum", tag=f"bank{bank}") for bank in (2, 4, 1, 3)]
+        z_turned = keep.tile([P, TURNED // UNIT, 2, P, 2], BF16, align_bytes=64)
 
         def turn(sources, adding):
             for u in range(2):
                 for b in range(2):
                     for e in range(2):
                         for n in range(2):
+                            unit = 2 * b + n
+                            first_unit, last_unit = (n == 0, n == 1) if u == 0 else (True, True)
                             nc.tensor.matmul(
-                                out=sum_banks[u][b][:, n, e, :],
-                                lhsT=sources[2 * u + e][:, cells(2 * b + n, 1)],
+                                out=early_sums[b][:, n, e, :] if u == 0 else late_sums[unit][:, 0, e, :],
+                                lhsT=sources[2 * u + e][:, cells(unit, 1)],
                                 rhs=ident[:],
                                 is_transpose=True,
-                                start=(not adding and e == 0 and n == 0),
-                                stop=(adding and e == 1 and n == 1),
+                                start=(not adding and e == 0 and first_unit),
+                                stop=(adding and e == 1 and last_unit),
                             )
 
-        def round_pair(u, b):
-            on_scalar(
-                out=z_turned[b][:].rearrange("q (n u p e) -> q u n p e", n=2, u=2, e=2)[:, u],
-                in_=sum_banks[u][b][:].rearrange("q n e p -> q n p e"),
-            )
+        def round_pair(u, first_unit, sums):
+            units = sums.shape[1]
+            on_scalar(out=z_turned[:, first_unit : first_unit + units, u], in_=sums[:].rearrange("q n e p -> q n p e"))
 
-        def turn_back(back, b, u):
-            words = z_turned[b][:].bitcast(F32)
-            for n in range(2):
-                nc.tensor.transpose(back[:, n, u, :], words[:, (2 * n + u) * P : (2 * n + u + 1) * P], ident[:])
+        def turn_back(back, unit, u):
+            words = z_turned[:, unit, u].rearrange("q p e -> q (p e)").bitcast(F32)
+            nc.tensor.transpose(back[:, u, :], words, ident[:])
 
-        def weave_words(back, b, n0, n1):
+        def weave_words(back, unit):
             on_scalar(
-                out=woven(cells(2 * b + n0, n1 - n0)).bitcast(F32).rearrange("p (n q u) -> p n q u", q=UNIT, u=2),
-                in_=back[:, n0:n1].rearrange("p n u q -> p n q u"),
+                out=woven(cells(unit, 1)).bitcast(F32).rearrange("p (q u) -> p q u", u=2),
+                in_=back[:].rearrange("p u q -> p q u"),
             )
 
         def quantise_z(cols):
@@ -260,28 +265,27 @@ def tile_picked_unet_none_p_kernel(
         turn(skip_sb, adding=False)
         turn(up, adding=True)
         for b in range(2):
-            round_pair(0, b)
-        for cols in high_blocks:
-            for t in (3, 2):
+            round_pair(0, 2 * b, early_sums[b])
+        for t in (2, 3):
+            for cols in high_blocks:
                 add_skip(nc.vector, t, cols)
-        for b in range(2):
-            round_pair(1, b)
-        backs = [psum.tile([P, 2, 2, P], F32, name="back_bank", tag=f"bank{bank}") for bank in (1, 3)]
-        for u in range(2):
-            for b in range(2):
-                turn_back(backs[b], b, u)
+        for unit, sums in enumerate(late_sums):
+            round_pair(1, unit, sums)
+        backs = [psum.tile([P, 2, P], F32, name="back_bank", tag=f"bank{bank}") for bank in (5, 6, 2, 4)]
+        for unit, back in enumerate(backs):
+            for u in range(2):
+                turn_back(back, unit, u)
         for cols in high_blocks:
             weave_planes(cols)
-        weave_words(backs[0], 0, 0, 2)
-        for n in range(2):
-            weave_words(backs[1], 1, n, n + 1)
+        for unit, back in enumerate(backs):
+            weave_words(back, unit)
 
         order = (
-            (high_blocks[0], 4, on_scalar),
-            (high_blocks[1], 1, on_scalar),
-            (cells(0, 2), 5, on_vector),
-            (cells(2, 1), 6, on_scalar),
-            (cells(3, 1), 7, on_vector),
+            (high_blocks[0], 3, on_scalar),
+            (high_blocks[1], 5, on_scalar),
+            (cells(0, 2), 7, on_vector),
+            (cells(2, 1), 0, on_scalar),
+            (cells(3, 1), 1, on_vector),
         )
         for cols, bank, mover in order:
             quantise_z(cols)

@@ -21,13 +21,11 @@ PACK = 4
 K_PASSES = K // (P * PACK)
 HALF = S // 2
 LIST_COLS = S // 16
-SCALE_ROWS = 16
 UNIT = 128
 BLOCK = 2 * UNIT
 TURNED = 2 * BLOCK
 LINE = 4
 W1_VECTOR = 80
-EARLY_SCALE_LOADS = 5
 
 
 def tile_picked_unet_none_p_kernel(
@@ -42,25 +40,24 @@ def tile_picked_unet_none_p_kernel(
         offs_sb = lists.tile([P, LIST_COLS], U16, name="offs_sb")
         cell_sb = lists.tile([P, LIST_COLS], U16, name="cell_sb")
 
-        x_table = [keep.tile([P, T], U32, name=f"x_table{g}", align_bytes=64) for g in range(K_PASSES)]
-        xs_table = keep.tile([P, T], U8, align_bytes=64)
+        x_table = [keep.tile([P, T], U32, name="x_table0", align_bytes=64)]
+        xs_table = keep.tile([P, T], U8, tag="first", align_bytes=64)
+        xs_placed = keep.tile([P, K_PASSES, S], U8, align_bytes=64)
         x_picked = [keep.tile([P, S], U32, name=f"x_picked{g}", align_bytes=64) for g in range(K_PASSES)]
         xs_picked = keep.tile([P, S], U8, align_bytes=64)
-        w1_raw = [keep.tile([P, PACK, H], F32, name=f"w1_raw{g}", align_bytes=64) for g in range(K_PASSES)]
+        w1_raw = [keep.tile([P, PACK, H], F32, name="w1_raw", tag=f"w1_raw{g}", align_bytes=64) for g in range(K_PASSES)]
         w1_codes = [keep.tile([P, H], U32, name=f"w1_codes{g}", align_bytes=64) for g in range(K_PASSES)]
         w1_scales = [keep.tile([P, H], U8, name=f"w1_scales{g}", align_bytes=64) for g in range(K_PASSES)]
-        skip_all = keep.tile([P, PACK, U], F32, align_bytes=64)
-        skip_sb = [skip_all[:, t, :] for t in range(PACK)]
         up = [keep.tile([P, U], F32, name=f"up{t}", align_bytes=64) for t in range(PACK)]
         z_planes = keep.tile([P, (U - TURNED) // BLOCK, PACK, BLOCK], BF16, align_bytes=64)
         ident = keep.tile([P, P], F32, align_bytes=64)
-        w2_codes = keep.tile([P, N], U32, align_bytes=64)
-        w2_scale_sb = keep.tile([P, N], U8, align_bytes=64)
 
         nc.vector.memset(xs_table[:].bitcast(I32), 0)
-        for t in range(PACK):
+        for t in (0, 1):
             nc.vector.memset(up[t][:].bitcast(I32), 0)
-        nc.vector.memset(w2_scale_sb[:].bitcast(I32), 0)
+        for t in (2, 3):
+            nc.scalar.copy(out=up[t][:], in_=up[0][:])
+        nc.vector.memset(xs_placed[:].rearrange("p g n -> p (g n)").bitcast(I32), 0)
         make_identity(nc, ident[:])
 
         w1_rows = w1.rearrange("(g p j) c -> g p j c", g=K_PASSES, j=PACK)
@@ -68,27 +65,13 @@ def tile_picked_unet_none_p_kernel(
         xs_rows = x_scales.bitcast(I32)
         skip_rows = skip.rearrange("(p t) v -> p t v", t=PACK)
 
-        def load_scales(n):
-            r, g = divmod(n, K_PASSES)
-            nc.sync.dma_start(out=xs_table[4 * g + r : P : 32, :].bitcast(I32), in_=xs_rows[g, r:SCALE_ROWS:4, :])
-
         nc.sync.dma_start(out=w1_raw[0][:], in_=w1_rows[0])
         nc.sync.dma_start(offs_sb[:], offs)
-        for n in range(EARLY_SCALE_LOADS):
-            load_scales(n)
+        for g in range(K_PASSES):
+            nc.sync.dma_start(out=xs_table[4 * g : P : 8, :].bitcast(I32), in_=xs_rows[g])
         nc.sync.dma_start(out=x_table[0][:].bitcast(I32), in_=x_rows[0])
-        for n in range(EARLY_SCALE_LOADS, 4 * K_PASSES):
-            load_scales(n)
         nc.sync.dma_start(cell_sb[:], cell)
         nc.sync.dma_start(out=w1_raw[1][:], in_=w1_rows[1])
-        nc.sync.dma_start(out=x_table[1][:].bitcast(I32), in_=x_rows[1])
-        nc.sync.dma_start(out=skip_all[:], in_=skip_rows)
-        nc.sync.dma_start(out=w2_codes[:].bitcast(I32), in_=w2_words[0].rearrange("p n t -> p (n t)").bitcast(I32))
-        for q in range(4):
-            nc.sync.dma_start(
-                out=w2_scale_sb[32 * q : 32 * q + 4, :].bitcast(I32),
-                in_=w2_scales[0, 4 * q : 4 * q + 4, :].bitcast(I32),
-            )
 
         on_scalar, on_vector = nc.scalar.copy, nc.vector.tensor_copy
 
@@ -100,7 +83,7 @@ def tile_picked_unet_none_p_kernel(
             return tile[:, part.start // 16 : part.stop // 16]
 
         def quantise_w1(g):
-            grouped = keep.tile([P, H * PACK], BF16, name=f"w1_bf{g}", align_bytes=64)
+            grouped = keep.tile([P, H * PACK], BF16, name="grouped", tag=("first", "second")[g], align_bytes=64)
             dealt = grouped[:].rearrange("p (t m j) -> p m j t", t=PACK, j=PACK)
             raw = w1_raw[g][:].rearrange("p j (m t) -> p m j t", t=PACK)
             on_vector(out=dealt[:, :W1_VECTOR], in_=raw[:, :W1_VECTOR])
@@ -117,16 +100,33 @@ def tile_picked_unet_none_p_kernel(
                 lhsT=w1_codes[g][:, cols].bitcast(FP8X4),
                 lhsT_scale=w1_scales[g][:, cols],
                 rhs=x_picked[g][:, part].bitcast(FP8X4),
-                rhs_scale=xs_picked[4 * g : P, part],
+                rhs_scale=xs_placed[:, g, part],
                 start=start,
                 stop=stop,
             )
 
+        nc.vector.tensor_copy(xs_picked[:], xs_table[:].indirect(offs_sb[:]))
+        for q in range(4):
+            nc.sync.dma_start(
+                out=xs_placed[32 * q : 32 * q + 4].bitcast(I32), in_=xs_picked[32 * q : 32 * q + 32 : 4, :].bitcast(I32)
+            )
         quantise_w1(0)
+        x_table.append(keep.tile([P, T], U32, name="x_table1", tag="w1_raw0", align_bytes=64))
+        nc.sync.dma_start(out=x_table[1][:].bitcast(I32), in_=x_rows[1])
+        skip_all = keep.tile([P, PACK, U], F32, tag="first", align_bytes=64)
+        skip_sb = [skip_all[:, t, :] for t in range(PACK)]
+        nc.sync.dma_start(out=skip_all[:], in_=skip_rows)
         gather_words(0, whole)
-        for part in halves:
-            nc.vector.tensor_copy(xs_picked[:, part], xs_table[:].indirect(list_part(offs_sb, part)))
         quantise_w1(1)
+        w2_codes = keep.tile([P, N], U32, tag="w1_raw1", align_bytes=64)
+        w2_scale_sb = keep.tile([P, N], U8, tag="second", align_bytes=64)
+        nc.sync.dma_start(out=w2_codes[:].bitcast(I32), in_=w2_words[0].rearrange("p n t -> p (n t)").bitcast(I32))
+        nc.gpsimd.memset(w2_scale_sb[:].bitcast(I32), 0)
+        for q in range(4):
+            nc.sync.dma_start(
+                out=w2_scale_sb[32 * q : 32 * q + 4, :].bitcast(I32),
+                in_=w2_scales[0, 4 * q : 4 * q + 4, :].bitcast(I32),
+            )
         for part in (first, second, halves[1]):
             gather_words(1, part)
 

@@ -26,6 +26,9 @@ BLOCK = 2 * UNIT
 TURNED = 2 * BLOCK
 LINE = 4
 W1_VECTOR = 80
+ROUNDED_AT = PACK * U * 4 - T // 2
+LAST_WORDS_AT = ROUNDED_AT + H * PACK * 2
+SCALE_TABLE_AT = LAST_WORDS_AT - T // 2
 
 
 def tile_picked_unet_none_p_kernel(
@@ -35,13 +38,14 @@ def tile_picked_unet_none_p_kernel(
     with ExitStack() as ctx:
         lists = ctx.enter_context(tc.tile_pool(name="lists", bufs=1))
         keep = ctx.enter_context(tc.tile_pool(name="keep", bufs=1))
+        shared = ctx.enter_context(tc.tile_pool(name="shared", bufs=1))
         psum = ctx.enter_context(tc.psum_pool(name="psum", bufs=1))
 
         offs_sb = lists.tile([P, LIST_COLS], U16, name="offs_sb")
         cell_sb = lists.tile([P, LIST_COLS], U16, name="cell_sb")
 
         x_table = [keep.tile([P, T], U32, name="x_table0", align_bytes=64)]
-        xs_table = keep.tile([P, T], U8, tag="first", align_bytes=64)
+        xs_table = shared.tile([P, T], U8, offset=SCALE_TABLE_AT, align_bytes=64)
         xs_placed = keep.tile([P, K_PASSES, S], U8, align_bytes=64)
         x_picked = [keep.tile([P, S], U32, name=f"x_picked{g}", align_bytes=64) for g in range(K_PASSES)]
         xs_picked = keep.tile([P, S], U8, align_bytes=64)
@@ -67,8 +71,7 @@ def tile_picked_unet_none_p_kernel(
 
         nc.sync.dma_start(out=w1_raw[0][:], in_=w1_rows[0])
         nc.sync.dma_start(offs_sb[:], offs)
-        for g in range(K_PASSES):
-            nc.sync.dma_start(out=xs_table[4 * g : P : 8, :].bitcast(I32), in_=xs_rows[g])
+        nc.sync.dma_start(out=xs_table[0:P:4, :].bitcast(I32), in_=xs_rows.rearrange("g m n -> m g n"))
         nc.sync.dma_start(out=x_table[0][:].bitcast(I32), in_=x_rows[0])
         nc.sync.dma_start(cell_sb[:], cell)
         nc.sync.dma_start(out=w1_raw[1][:], in_=w1_rows[1])
@@ -82,8 +85,7 @@ def tile_picked_unet_none_p_kernel(
         def list_part(tile, part):
             return tile[:, part.start // 16 : part.stop // 16]
 
-        def quantise_w1(g):
-            grouped = keep.tile([P, H * PACK], BF16, name="grouped", tag=("first", "second")[g], align_bytes=64)
+        def quantise_w1(g, grouped):
             dealt = grouped[:].rearrange("p (t m j) -> p m j t", t=PACK, j=PACK)
             raw = w1_raw[g][:].rearrange("p j (m t) -> p m j t", t=PACK)
             on_vector(out=dealt[:, :W1_VECTOR], in_=raw[:, :W1_VECTOR])
@@ -106,18 +108,18 @@ def tile_picked_unet_none_p_kernel(
             )
 
         nc.vector.tensor_copy(xs_picked[:], xs_table[:].indirect(offs_sb[:]))
-        for q in range(4):
+        for q in (0, 2, 1, 3):
             nc.sync.dma_start(
                 out=xs_placed[32 * q : 32 * q + 4].bitcast(I32), in_=xs_picked[32 * q : 32 * q + 32 : 4, :].bitcast(I32)
             )
-        quantise_w1(0)
-        x_table.append(keep.tile([P, T], U32, name="x_table1", tag="w1_raw0", align_bytes=64))
+        x_table.append(shared.tile([P, T], U32, name="x_table1", offset=LAST_WORDS_AT, align_bytes=64))
         nc.sync.dma_start(out=x_table[1][:].bitcast(I32), in_=x_rows[1])
-        skip_all = keep.tile([P, PACK, U], F32, tag="first", align_bytes=64)
+        quantise_w1(0, shared.tile([P, H * PACK], BF16, name="w1_bf0", offset=ROUNDED_AT, align_bytes=64))
+        skip_all = shared.tile([P, PACK, U], F32, offset=0, align_bytes=64)
         skip_sb = [skip_all[:, t, :] for t in range(PACK)]
         nc.sync.dma_start(out=skip_all[:], in_=skip_rows)
         gather_words(0, whole)
-        quantise_w1(1)
+        quantise_w1(1, keep.tile([P, H * PACK], BF16, name="w1_bf1", tag="second", align_bytes=64))
         w2_codes = keep.tile([P, N], U32, tag="w1_raw1", align_bytes=64)
         w2_scale_sb = keep.tile([P, N], U8, tag="second", align_bytes=64)
         nc.sync.dma_start(out=w2_codes[:].bitcast(I32), in_=w2_words[0].rearrange("p n t -> p (n t)").bitcast(I32))
@@ -266,9 +268,9 @@ def tile_picked_unet_none_p_kernel(
         turn(up, adding=True)
         for b in range(2):
             round_pair(0, 2 * b, early_sums[b])
-        for t in (2, 3):
-            for cols in high_blocks:
-                add_skip(nc.vector, t, cols)
+        add_skip(nc.vector, 2, slice(TURNED, U))
+        for cols in high_blocks:
+            add_skip(nc.vector, 3, cols)
         for unit, sums in enumerate(late_sums):
             round_pair(1, unit, sums)
         backs = [psum.tile([P, 2, P], F32, name="back_bank", tag=f"bank{bank}") for bank in (5, 6, 2, 4)]

@@ -26,8 +26,11 @@ BLOCK = 2 * UNIT
 TURNED = 2 * BLOCK
 LINE = 4
 W1_VECTOR = 80
-ROUNDED_AT = PACK * U * 4 - T // 2
-LAST_WORDS_AT = ROUNDED_AT + H * PACK * 2
+ROUNDED_BYTES = H * PACK * 2
+W2_CODES_AT = PACK * U * 4
+W2_SCALES_AT = W2_CODES_AT + N * 4
+ROUNDED_AT = W2_CODES_AT + ROUNDED_BYTES // 2, W2_CODES_AT - ROUNDED_BYTES // 2
+LAST_WORDS_AT = ROUNDED_AT[0] + ROUNDED_BYTES
 SCALE_TABLE_AT = LAST_WORDS_AT - T // 2
 
 
@@ -114,14 +117,19 @@ def tile_picked_unet_none_p_kernel(
             )
         x_table.append(shared.tile([P, T], U32, name="x_table1", offset=LAST_WORDS_AT, align_bytes=64))
         nc.sync.dma_start(out=x_table[1][:].bitcast(I32), in_=x_rows[1])
-        quantise_w1(0, shared.tile([P, H * PACK], BF16, name="w1_bf0", offset=ROUNDED_AT, align_bytes=64))
+        quantise_w1(0, shared.tile([P, H * PACK], BF16, name="w1_bf0", offset=ROUNDED_AT[0], align_bytes=64))
+        gather_words(0, whole)
+        quantise_w1(1, shared.tile([P, H * PACK], BF16, name="w1_bf1", offset=ROUNDED_AT[1], align_bytes=64))
         skip_all = shared.tile([P, PACK, U], F32, offset=0, align_bytes=64)
         skip_sb = [skip_all[:, t, :] for t in range(PACK)]
-        nc.sync.dma_start(out=skip_all[:], in_=skip_rows)
-        gather_words(0, whole)
-        quantise_w1(1, keep.tile([P, H * PACK], BF16, name="w1_bf1", tag="second", align_bytes=64))
-        w2_codes = keep.tile([P, N], U32, tag="w1_raw1", align_bytes=64)
-        w2_scale_sb = keep.tile([P, N], U8, tag="second", align_bytes=64)
+        for planes, cols in (
+            (slice(0, PACK), slice(0, TURNED)),
+            (slice(0, 2), slice(TURNED, U)),
+            (slice(2, PACK), slice(TURNED, U)),
+        ):
+            nc.sync.dma_start(out=skip_all[:, planes, cols], in_=skip_rows[:, planes, cols])
+        w2_codes = shared.tile([P, N], U32, offset=W2_CODES_AT, align_bytes=64)
+        w2_scale_sb = shared.tile([P, N], U8, offset=W2_SCALES_AT, align_bytes=64)
         nc.sync.dma_start(out=w2_codes[:].bitcast(I32), in_=w2_words[0].rearrange("p n t -> p (n t)").bitcast(I32))
         nc.gpsimd.memset(w2_scale_sb[:].bitcast(I32), 0)
         for q in range(4):

@@ -183,12 +183,12 @@ def tile_picked_unet_none_p_kernel(
         for t in vector_planes:
             leave_psum(on_vector, t, halves[0])
         scatter_vector(1, halves[0])
-        leave_psum(on_scalar, 1, halves[1])
         for t in scalar_planes:
             leave_psum(on_scalar, t, rest)
         for t in scalar_planes:
             scatter_scalar(t, rest)
-        leave_psum(on_vector, 2, halves[1])
+        for t in vector_planes:
+            leave_psum(on_vector, t, halves[1])
         scatter_vector(1, halves[1])
         scatter_vector(2, whole)
 
@@ -223,7 +223,7 @@ def tile_picked_unet_none_p_kernel(
         def turn(sources, adding):
             for u in range(2):
                 for b in range(2):
-                    for e in range(2):
+                    for e in (1, 0):
                         for n in range(2):
                             unit = 2 * b + n
                             first_unit, last_unit = (n == 0, n == 1) if u == 0 else (True, True)
@@ -232,8 +232,8 @@ def tile_picked_unet_none_p_kernel(
                                 lhsT=sources[2 * u + e][:, cells(unit, 1)],
                                 rhs=ident[:],
                                 is_transpose=True,
-                                start=(not adding and e == 0 and first_unit),
-                                stop=(adding and e == 1 and last_unit),
+                                start=(not adding and e == 1 and first_unit),
+                                stop=(adding and e == 0 and last_unit),
                             )
 
         def round_pair(u, first_unit, sums):
@@ -276,9 +276,9 @@ def tile_picked_unet_none_p_kernel(
         turn(up, adding=True)
         for b in range(2):
             round_pair(0, 2 * b, early_sums[b])
-        add_skip(nc.vector, 2, slice(TURNED, U))
+        add_skip(nc.vector, 3, slice(TURNED, U))
         for cols in high_blocks:
-            add_skip(nc.vector, 3, cols)
+            add_skip(nc.vector, 2, cols)
         for unit, sums in enumerate(late_sums):
             round_pair(1, unit, sums)
         backs = [psum.tile([P, 2, P], F32, name="back_bank", tag=f"bank{bank}") for bank in (5, 6, 2, 4)]

from contextlib import ExitStack

import concourse.mybir as mybir
from concourse.masks import make_identity

K, T, S, H, N, U = 1024, 2048, 512, 512, 128, 1024
FLOPS = 2 * K * H * S + 2 * H * N * U

F32 = mybir.dt.float32
BF16 = mybir.dt.bfloat16
I32 = mybir.dt.int32
U32 = mybir.dt.uint32
U16 = mybir.dt.uint16
U8 = mybir.dt.uint8
FP8X4 = mybir.dt.float8_e4m3fn_x4
COPY = mybir.ActivationFunctionType.Copy
ADD = mybir.AluOpType.add

P = 128
PACK = 4
K_PASSES = K // (P * PACK)
HALF = S // 2
LIST_COLS = S // 16
UNIT = 128
BLOCK = 2 * UNIT
TURNED = 2 * BLOCK
LINE = 4
W1_VECTOR = 80
ROUNDED_BYTES = H * PACK * 2
W2_CODES_AT = PACK * U * 4
W2_SCALES_AT = W2_CODES_AT + N * 4
ROUNDED_AT = W2_CODES_AT + ROUNDED_BYTES // 2, W2_CODES_AT - ROUNDED_BYTES // 2
LAST_WORDS_AT = ROUNDED_AT[0] + ROUNDED_BYTES
SCALE_TABLE_AT = LAST_WORDS_AT - T // 2


def tile_picked_unet_none_p_kernel(
    tc, x_words, x_scales, w1, w2_words, w2_scales, skip, offs, cell, out
):
    nc = tc.nc
    with ExitStack() as ctx:
        lists = ctx.enter_context(tc.tile_pool(name="lists", bufs=1))
        keep = ctx.enter_context(tc.tile_pool(name="keep", bufs=1))
        shared = ctx.enter_context(tc.tile_pool(name="shared", bufs=1))
        psum = ctx.enter_context(tc.psum_pool(name="psum", bufs=1))

        offs_sb = lists.tile([P, LIST_COLS], U16, name="offs_sb")
        cell_sb = lists.tile([P, LIST_COLS], U16, name="cell_sb")

        x_table = [keep.tile([P, T], U32, name="x_table0", align_bytes=64)]
        xs_table = shared.tile([P, T], U8, offset=SCALE_TABLE_AT, align_bytes=64)
        xs_placed = keep.tile([P, K_PASSES, S], U8, align_bytes=64)
        x_picked = [keep.tile([P, S], U32, name=f"x_picked{g}", align_bytes=64) for g in range(K_PASSES)]
        xs_picked = keep.tile([P, S], U8, align_bytes=64)
        w1_raw = [keep.tile([P, PACK, H], F32, name="w1_raw", tag=f"w1_raw{g}", align_bytes=64) for g in range(K_PASSES)]
        w1_codes = [keep.tile([P, H], U32, name=f"w1_codes{g}", align_bytes=64) for g in range(K_PASSES)]
        w1_scales = [keep.tile([P, H], U8, name=f"w1_scales{g}", align_bytes=64) for g in range(K_PASSES)]
        up = [keep.tile([P, U], F32, name=f"up{t}", align_bytes=64) for t in range(PACK)]
        z_planes = keep.tile([P, (U - TURNED) // BLOCK, PACK, BLOCK], BF16, align_bytes=64)
        ident = keep.tile([P, P], F32, align_bytes=64)

        nc.vector.memset(xs_table[:].bitcast(I32), 0)
        for t in (0, 1):
            nc.vector.memset(up[t][:].bitcast(I32), 0)
        for t in (2, 3):
            nc.scalar.copy(out=up[t][:], in_=up[0][:])
        nc.vector.memset(xs_placed[:].rearrange("p g n -> p (g n)").bitcast(I32), 0)
        make_identity(nc, ident[:])

        w1_rows = w1.rearrange("(g p j) c -> g p j c", g=K_PASSES, j=PACK)
        x_rows = x_words.rearrange("g p n t -> g p (n t)").bitcast(I32)
        xs_rows = x_scales.bitcast(I32)
        skip_rows = skip.rearrange("(p t) v -> p t v", t=PACK)

        nc.sync.dma_start(out=w1_raw[0][:], in_=w1_rows[0])
        nc.sync.dma_start(offs_sb[:], offs)
        nc.sync.dma_start(out=xs_table[0:P:4, :].bitcast(I32), in_=xs_rows.rearrange("g m n -> m g n"))
        nc.sync.dma_start(out=x_table[0][:].bitcast(I32), in_=x_rows[0])
        nc.sync.dma_start(cell_sb[:], cell)
        nc.sync.dma_start(out=w1_raw[1][:], in_=w1_rows[1])

        on_scalar, on_vector = nc.scalar.copy, nc.vector.tensor_copy

        whole = slice(0, S)
        halves = slice(0, HALF), slice(HALF, S)
        first, second, rest = slice(0, P), slice(P, HALF), slice(P, S)

        def list_part(tile, part):
            return tile[:, part.start // 16 : part.stop // 16]

        def quantise_w1(g, grouped):
            dealt = grouped[:].rearrange("p (t m j) -> p m j t", t=PACK, j=PACK)
            raw = w1_raw[g][:].rearrange("p j (m t) -> p m j t", t=PACK)
            on_vector(out=dealt[:, :W1_VECTOR], in_=raw[:, :W1_VECTOR])
            on_scalar(out=dealt[:, W1_VECTOR:], in_=raw[:, W1_VECTOR:])
            nc.vector.quantize_mx(out=w1_codes[g][:].bitcast(FP8X4), scales=w1_scales[g][:], in_=grouped[:])

        def gather_words(g, part):
            nc.vector.tensor_copy(x_picked[g][:, part], x_table[g][:].indirect(list_part(offs_sb, part)))

        def first_product(t, part, acc, g, start, stop):
            cols = slice(t * P, (t + 1) * P)
            nc.tensor.matmul_mx(
                out=acc,
                lhsT=w1_codes[g][:, cols].bitcast(FP8X4),
                lhsT_scale=w1_scales[g][:, cols],
                rhs=x_picked[g][:, part].bitcast(FP8X4),
                rhs_scale=xs_placed[:, g, part],
                start=start,
                stop=stop,
            )

        nc.vector.tensor_copy(xs_picked[:], xs_table[:].indirect(offs_sb[:]))
        for q in (0, 2, 1, 3):
            nc.sync.dma_start(
                out=xs_placed[32 * q : 32 * q + 4].bitcast(I32), in_=xs_picked[32 * q : 32 * q + 32 : 4, :].bitcast(I32)
            )
        x_table.append(shared.tile([P, T], U32, name="x_table1", offset=LAST_WORDS_AT, align_bytes=64))
        nc.sync.dma_start(out=x_table[1][:].bitcast(I32), in_=x_rows[1])
        quantise_w1(0, shared.tile([P, H * PACK], BF16, name="w1_bf0", offset=ROUNDED_AT[0], align_bytes=64))
        gather_words(0, whole)
        quantise_w1(1, shared.tile([P, H * PACK], BF16, name="w1_bf1", offset=ROUNDED_AT[1], align_bytes=64))
        skip_all = shared.tile([P, PACK, U], F32, offset=0, align_bytes=64)
        skip_sb = [skip_all[:, t, :] for t in range(PACK)]
        for planes, cols in (
            (slice(0, PACK), slice(0, TURNED)),
            (slice(0, 2), slice(TURNED, U)),
            (slice(2, PACK), slice(TURNED, U)),
        ):
            nc.sync.dma_start(out=skip_all[:, planes, cols], in_=skip_rows[:, planes, cols])
        w2_codes = shared.tile([P, N], U32, offset=W2_CODES_AT, align_bytes=64)
        w2_scale_sb = shared.tile([P, N], U8, offset=W2_SCALES_AT, align_bytes=64)
        nc.sync.dma_start(out=w2_codes[:].bitcast(I32), in_=w2_words[0].rearrange("p n t -> p (n t)").bitcast(I32))
        nc.gpsimd.memset(w2_scale_sb[:].bitcast(I32), 0)
        for q in range(4):
            nc.sync.dma_start(
                out=w2_scale_sb[32 * q : 32 * q + 4, :].bitcast(I32),
                in_=w2_scales[0, 4 * q : 4 * q + 4, :].bitcast(I32),
            )
        for part in (first, second, halves[1]):
            gather_words(1, part)

        scalar_planes, vector_planes = (0, 3), (1, 2)
        starters = [psum.tile([P, P], F32, name="h_acc", tag=f"bank{bank}") for bank in (0, 7)]
        held = [(0, rest), (1, halves[0]), (1, halves[1]), (2, halves[0]), (2, halves[1]), (3, rest)]
        accs = [
            psum.tile([P, span.stop - span.start], F32, name="h_acc", tag=f"bank{n + 1}")
            for n, (t, span) in enumerate(held)
        ]
        steps = [
            (1, halves[0]), (3, halves[0]), (0, second), (5, second),
            (2, halves[1]), (4, halves[1]), (0, halves[1]), (5, halves[1]),
        ]
        for g in range(K_PASSES):
            for starter, t in zip(starters, scalar_planes):
                first_product(t, first, starter[:], g, g == 0, g == K_PASSES - 1)
            for n, part in steps:
                t, span = held[n]
                first_product(
                    t,
                    part,
                    accs[n][:, part.start - span.start : part.stop - span.start],
                    g,
                    g == 0 and part.start == span.start,
                    g == K_PASSES - 1 and part.stop == span.stop,
                )

        h = [keep.tile([P, S], F32, name=f"h{t}", align_bytes=64) for t in range(PACK)]

        def scatter_vector(t, part):
            nc.vector.tensor_copy(up[t][:].indirect(list_part(cell_sb, part)), h[t][:, part])

        def scatter_scalar(t, part):
            nc.scalar.activation(up[t][:].indirect(list_part(cell_sb, part)), h[t][:, part], COPY)

        def leave_psum(mover, t, part):
            mover(out=h[t][:, part], in_=accs[held.index((t, part))][:])

        for t, starter in zip(scalar_planes, starters):
            on_scalar(out=h[t][:, first], in_=starter[:])
        for t in scalar_planes:
            scatter_scalar(t, first)
        for t in vector_planes:
            leave_psum(on_vector, t, halves[0])
        scatter_vector(1, halves[0])
        for t in scalar_planes:
            leave_psum(on_scalar, t, rest)
        for t in scalar_planes:
            scatter_scalar(t, rest)
        for t in vector_planes:
            leave_psum(on_vector, t, halves[1])
        scatter_vector(1, halves[1])
        scatter_vector(2, whole)

        z_bf = keep.tile([P, U * PACK], BF16, align_bytes=64)
        z_codes = keep.tile([P, U], U32, align_bytes=64)
        z_scales = keep.tile([P, U], U8, align_bytes=64)

        def cells(first_unit, units):
            return slice(first_unit * UNIT, (first_unit + units) * UNIT)

        def woven(cols):
            return z_bf[:, cols.start * PACK : cols.stop * PACK]

        def add_skip(engine, t, cols):
            engine.tensor_tensor(
                z_planes[:, (cols.start - TURNED) // BLOCK : (cols.stop - TURNED) // BLOCK, t, :],
                up[t][:, cols].rearrange("p (n v) -> p n v", v=BLOCK),
                skip_sb[t][:, cols].rearrange("p (n v) -> p n v", v=BLOCK),
                ADD,
            )

        def weave_planes(cols):
            on_vector(
                out=woven(cols).rearrange("p (c i t) -> p c t i", i=LINE, t=PACK),
                in_=z_planes[:, (cols.start - TURNED) // BLOCK].rearrange("p t (c i) -> p c t i", i=LINE),
            )

        early_sums = [psum.tile([P, 2, 2, P], F32, name="early_sum", tag=f"bank{bank}") for bank in (7, 0)]
        late_sums = [psum.tile([P, 1, 2, P], F32, name="late_sum", tag=f"bank{bank}") for bank in (2, 4, 1, 3)]
        z_turned = keep.tile([P, TURNED // UNIT, 2, P, 2], BF16, align_bytes=64)

        def turn(sources, adding):
            for u in range(2):
                for b in range(2):
                    for e in (1, 0):
                        for n in range(2):
                            unit = 2 * b + n
                            first_unit, last_unit = (n == 0, n == 1) if u == 0 else (True, True)
                            nc.tensor.matmul(
                                out=early_sums[b][:, n, e, :] if u == 0 else late_sums[unit][:, 0, e, :],
                                lhsT=sources[2 * u + e][:, cells(unit, 1)],
                                rhs=ident[:],
                                is_transpose=True,
                                start=(not adding and e == 1 and first_unit),
                                stop=(adding and e == 0 and last_unit),
                            )

        def round_pair(u, first_unit, sums):
            units = sums.shape[1]
            on_scalar(out=z_turned[:, first_unit : first_unit + units, u], in_=sums[:].rearrange("q n e p -> q n p e"))

        def turn_back(back, unit, u):
            words = z_turned[:, unit, u].rearrange("q p e -> q (p e)").bitcast(F32)
            nc.tensor.transpose(back[:, u, :], words, ident[:])

        def weave_words(back, unit):
            on_scalar(
                out=woven(cells(unit, 1)).bitcast(F32).rearrange("p (q u) -> p q u", u=2),
                in_=back[:].rearrange("p u q -> p q u"),
            )

        def quantise_z(cols):
            nc.vector.quantize_mx(out=z_codes[:, cols].bitcast(FP8X4), scales=z_scales[:, cols], in_=woven(cols))

        def second_product(cols, bank, mover):
            width = cols.stop - cols.start
            acc = psum.tile([P, width], F32, name="out_acc", tag=f"bank{bank}")
            nc.tensor.matmul_mx(
                out=acc[:],
                lhsT=w2_codes[:].bitcast(FP8X4),
                lhsT_scale=w2_scale_sb[:],
                rhs=z_codes[:, cols].bitcast(FP8X4),
                rhs_scale=z_scales[:, cols],
                start=True,
                stop=True,
            )
            result = keep.tile([P, width], F32, name=f"result{cols.start}")
            mover(out=result[:], in_=acc[:])
            nc.sync.dma_start(out=out[:, cols], in_=result[:])

        high_blocks = cells(4, 2), cells(6, 2)
        for t in (1, 0):
            add_skip(nc.gpsimd, t, slice(TURNED, U))
        turn(skip_sb, adding=False)
        turn(up, adding=True)
        for b in range(2):
            round_pair(0, 2 * b, early_sums[b])
        add_skip(nc.vector, 3, slice(TURNED, U))
        for cols in high_blocks:
            add_skip(nc.vector, 2, cols)
        for unit, sums in enumerate(late_sums):
            round_pair(1, unit, sums)
        backs = [psum.tile([P, 2, P], F32, name="back_bank", tag=f"bank{bank}") for bank in (5, 6, 2, 4)]
        for unit, back in enumerate(backs):
            for u in range(2):
                turn_back(back, unit, u)
        for cols in high_blocks:
            weave_planes(cols)
        for unit, back in enumerate(backs):
            weave_words(back, unit)

        order = (
            (high_blocks[0], 3, on_scalar),
            (high_blocks[1], 5, on_scalar),
            (cells(0, 2), 7, on_vector),
            (cells(2, 1), 0, on_scalar),
            (cells(3, 1), 1, on_vector),
        )
        for cols, bank, mover in order:
            quantise_z(cols)
        for cols, bank, mover in order:
            second_product(cols, bank, mover)
